import numpy as np
import ml_dtypes


def mxq(x, axis, fmt="e4m3"):
    dtype, down = {"e4m3": (ml_dtypes.float8_e4m3fn, 7), "e5m2": (ml_dtypes.float8_e5m2, 14)}[fmt]
    v = np.moveaxis(np.asarray(x, np.float32).astype(ml_dtypes.bfloat16).astype(np.float64), axis, -1)
    blocks = v.reshape(v.shape[:-1] + (-1, 32))
    amax = np.abs(blocks).max(-1, keepdims=True)
    byte = np.maximum(np.where(amax > 0, np.frexp(amax)[1] - 1 + 127, 0) - down, 1)
    scale = np.exp2(byte - 127.0)
    codes = (blocks / scale).astype(np.float32).astype(dtype).astype(np.float64)
    return np.moveaxis((codes * scale).reshape(v.shape), -1, axis)


WIDE = False


def mx_kscale(k):
    if not WIDE:
        return np.ones(k)
    levels = np.array([10, -10, 5, -5, 0])
    if k % 512:
        return np.exp2(np.random.permutation(np.resize(levels, k // 32))).repeat(32)
    a = np.empty((k // 512, 16))
    for p in range(k // 512):
        a[p, :8] = np.random.permutation(np.resize(levels, 8))
        for g in range(8):
            far = levels[np.abs(levels - a[p, g]) >= 10]
            a[p, g + 8] = far[np.random.randint(len(far))]
    return np.exp2(a.ravel()).repeat(32)


BF16 = ml_dtypes.bfloat16


def bf(x):
    return np.asarray(x, np.float32).astype(BF16)


def f64(x):
    return np.asarray(x).astype(np.float64)


E2M1 = np.array([0.0, 0.5, 1.0, 1.5, 2.0, 3.0, 4.0, 6.0, -0.0, -0.5, -1.0, -1.5, -2.0, -3.0, -4.0, -6.0])


def pack_weight(w, fmt):
    k, n = w.shape
    w = f64(bf(w)).reshape(k // 32, 32, n)
    amax = np.abs(w).max(1)
    if fmt == "e4m3":
        byte = np.frexp(amax)[1] - 1 + 127 - 7
    else:
        mant, ex = np.frexp(amax / 6.0)
        byte = np.where(mant > 0.5, ex, ex - 1) + 127
    byte = np.clip(np.where(amax > 0, byte, 1), 1, 254)
    scaled = (w * np.exp2(127.0 - byte)[:, None, :]).reshape(k, n).astype(np.float32)
    by_word = np.ascontiguousarray(scaled.reshape(k // 512, 128, 4, n).transpose(0, 1, 3, 2))
    if fmt == "e4m3":
        words = by_word.astype(ml_dtypes.float8_e4m3fn).view(np.uint8)
    else:
        c = by_word.astype(ml_dtypes.float4_e2m1fn).view(np.uint8) & 0xF
        words = c[..., 0::2] | (c[..., 1::2] << 4)
    return np.ascontiguousarray(words), np.ascontiguousarray(byte.astype(np.uint8).reshape(k // 512, 16, n))


def unpack_weight(words, scales, fmt):
    g, p, n, _ = words.shape
    if fmt == "e4m3":
        vals = np.ascontiguousarray(words).view(ml_dtypes.float8_e4m3fn).astype(np.float64)
    else:
        nib = np.empty((g, p, n, 4), np.uint8)
        nib[..., 0::2] = words & 0xF
        nib[..., 1::2] = words >> 4
        vals = E2M1[nib]
    vals = vals * np.repeat(np.exp2(scales.astype(np.float64) - 127.0), 8, axis=1)[..., None]
    return vals.transpose(0, 1, 3, 2).reshape(g * 512, n)
def pack4(w):
    words, scales = pack_weight(w, "e2m1")
    return words.reshape(words.shape[0], 128, -1), scales


def unpack4(words, scales):
    return unpack_weight(words.reshape(words.shape[0], 128, -1, 2), scales, "e2m1")


def planes(Y):
    n, m = Y.shape
    b = f64(bf(Y)).reshape(n // 32, 32, m)
    amax = np.abs(b).max(1)
    byte = np.clip(np.where(amax > 0, np.frexp(amax)[1] - 1 + 127 - 7, 1), 1, 254)
    codes = (b * np.exp2(127.0 - byte)[:, None, :]).reshape(n, m).astype(np.float32).astype(ml_dtypes.float8_e4m3fn).view(np.uint8)
    words = codes.reshape(n // 512, 128, 4, m).transpose(0, 1, 3, 2)
    return np.ascontiguousarray(words), np.ascontiguousarray(byte.astype(np.uint8).reshape(n // 512, 16, m))


ROWS, BLK, REST = 1024, 1024, 1536


def setup_inputs():
    s = mx_kscale(BLK)[:, None]
    w = np.random.randn(BLK, ROWS)
    lost = np.where(np.abs(w) > 0.67, 0.1 * np.random.randn(BLK, ROWS), w)
    diag = np.exp(0.3 * np.random.randn(BLK, 1))
    f_words, f_scales = pack_weight(lost / diag * s, "e4m3")
    a_words, a_scales = pack4(2.0 * np.random.randn(BLK, REST) / np.sqrt(BLK) / s)
    b_words, b_scales = pack_weight(1.5 * np.random.randn(BLK, REST) / np.sqrt(BLK) / s, "e4m3")
    d = bf(np.exp(0.8 * np.random.randn(REST)))
    c = bf(1.5 * np.random.randn(BLK, REST) * f64(d) / np.sqrt(BLK) / s)
    v = bf(np.random.randn(ROWS, REST) * f64(d))
    return {"f_words": f_words, "f_scales": f_scales, "a_words": a_words, "a_scales": a_scales,
            "b_words": b_words, "b_scales": b_scales, "c": c, "d": d, "v": v}

def reference(f_words, f_scales, a_words, a_scales, b_words, b_scales, c, d, v):
    e = unpack_weight(f_words, f_scales, "e4m3").T
    a = unpack4(a_words, a_scales)
    b = unpack_weight(b_words, b_scales, "e4m3")
    cq = mxq(f64(c), 0, "e4m3")
    pa = e @ a
    pb = e @ b
    pc = e @ cq
    y = f64(v) - f64(d) * (pa + pb) - pc
    Y = y.T
    words, scales = planes(Y)
    return y, words, scales

@@ -1,0 +1,289 @@
+from contextlib import ExitStack
+
+import concourse.mybir as mybir
+from concourse.masks import make_identity
+
+ROWS, BLK, REST = 1024, 1024, 1536
+FLOPS = 3 * 2 * ROWS * BLK * REST
+
+F32 = mybir.dt.float32
+BF16 = mybir.dt.bfloat16
+I32 = mybir.dt.int32
+U32 = mybir.dt.uint32
+U8 = mybir.dt.uint8
+FP8X4 = mybir.dt.float8_e4m3fn_x4
+FP4X4 = mybir.dt.float4_e2m1fn_x4
+MULT = mybir.AluOpType.mult
+SUB = mybir.AluOpType.subtract
+
+P = 128
+NT = 512
+PASSES = BLK // 512
+MTILES = ROWS // P
+NTILES = REST // NT
+TILES = MTILES * NTILES
+LEAD = 6
+F_CHUNKS = [(0, 2), (2, 4), (4, 8)]
+V_HALF = 4
+
+
+def tile_lazy_pruning_update_k3_kernel(
+    tc, f_words, f_scales, a_words, a_scales, b_words, b_scales, c, d, v, out_0, out_1, out_2
+):
+    nc = tc.nc
+    with ExitStack() as ctx:
+        keep = ctx.enter_context(tc.tile_pool(name="keep", bufs=1))
+        work = ctx.enter_context(tc.tile_pool(name="work", bufs=1))
+        psum = ctx.enter_context(tc.psum_pool(name="psum", bufs=1))
+        ctx.enter_context(tc.manual_schedule())
+
+        def kept(name, shape, dtype):
+            return keep.tile(shape, dtype, name=name, align_bytes=64)
+
+        f_plane = kept("f_plane", [P, PASSES, ROWS], U8)
+        a_plane = kept("a_plane", [P, PASSES, REST], U8)
+        b_plane = kept("b_plane", [P, PASSES, REST], U8)
+        f_codes = [kept("f_codes%d" % lo, [P, PASSES, (hi - lo) * P], U32) for lo, hi in F_CHUNKS]
+        a_codes = [kept("a_codes%d" % n, [P, PASSES, 2 * NT], U8) for n in range(NTILES)]
+        b_codes = [kept("b_codes%d" % n, [P, PASSES, NT], U32) for n in range(NTILES)]
+        c_raw = [[kept("c_raw%d_%d" % (n, g), [P, 4, NT], BF16) for g in range(PASSES)] for n in range(NTILES)]
+        c_grp = [[kept("c_grp%d_%d" % (n, g), [P, NT, 4], BF16) for g in range(PASSES)] for n in range(NTILES)]
+        c_codes = [[kept("c_codes%d_%d" % (n, g), [P, NT], U32) for g in range(PASSES)] for n in range(NTILES)]
+        c_plane = [[kept("c_plane%d_%d" % (n, g), [P, NT], U8) for g in range(PASSES)] for n in range(NTILES)]
+        v_sb = [[kept("v%d_%d" % (n, h), [P, V_HALF, NT], BF16) for h in range(2)] for n in range(NTILES)]
+        d_col = kept("d_col", [P, NTILES, 4], BF16)
+        d_row = kept("d_row", [P, NTILES, NT], BF16)
+        ident = kept("ident", [P, P], F32)
+        y_codes = [kept("y_codes%d" % n, [P, ROWS], U32) for n in range(NTILES)]
+        y_plane = [kept("y_plane%d" % n, [P, ROWS], U8) for n in range(NTILES)]
+
+        f_view = f_words.rearrange("g p m t -> p g (m t)")
+        a_view = a_words.rearrange("g p x -> p g x")
+        b_view = b_words.rearrange("g p n t -> p g (n t)")
+
+        def load_scales(queue, plane, scales, first_row):
+            for q in range(4):
+                lo = 32 * q + first_row
+                queue.dma_start(
+                    out=plane[lo : lo + 4, :, :].bitcast(I32),
+                    in_=scales[:, 4 * q : 4 * q + 4, :].rearrange("g r n -> r g n").bitcast(I32),
+                )
+
+        def load_f(k):
+            lo, hi = F_CHUNKS[k]
+            nc.sync.dma_start(out=f_codes[k][:].bitcast(I32), in_=f_view[:, :, 4 * P * lo : 4 * P * hi].bitcast(I32))
+
+        def load_a(n):
+            nc.sync.dma_start(out=a_codes[n][:].bitcast(I32), in_=a_view[:, :, 2 * NT * n : 2 * NT * (n + 1)].bitcast(I32))
+
+        def load_b(n, g0, g1):
+            nc.sync.dma_start(
+                out=b_codes[n][:, g0:g1, :].bitcast(I32),
+                in_=b_view[:, g0:g1, 4 * NT * n : 4 * NT * (n + 1)].bitcast(I32),
+            )
+
+        def load_c(n, g):
+            rows = c[512 * g : 512 * (g + 1), NT * n : NT * (n + 1)]
+            nc.sync.dma_start(out=c_raw[n][g][:], in_=rows.rearrange("(p j) w -> p j w", j=4))
+
+        def load_v(n, h):
+            rows = v[V_HALF * P * h : V_HALF * P * (h + 1), NT * n : NT * (n + 1)]
+            nc.sync.dma_start(out=v_sb[n][h][:], in_=rows.rearrange("(m p) w -> p m w", p=P))
+
+        nc.gpsimd.dma_start(out=d_col[:], in_=d.rearrange("(n p t) -> p n t", p=P, t=4))
+        for plane in (f_plane, b_plane, a_plane):
+            nc.vector.memset(plane[:].rearrange("p g n -> p (g n)").bitcast(I32), 0)
+        make_identity(nc, ident[:])
+
+        load_f(0)
+        load_b(0, 0, 1)
+        load_scales(nc.sync, f_plane, f_scales, 0)
+        load_scales(nc.sync, b_plane, b_scales, 4)
+        load_b(0, 1, 2)
+        load_a(0)
+        load_scales(nc.sync, a_plane, a_scales, 0)
+        load_f(1)
+        load_c(0, 0)
+        load_c(0, 1)
+        load_f(2)
+        load_b(1, 0, 2)
+        load_a(1)
+        load_v(0, 0)
+        load_c(1, 0)
+        load_v(0, 1)
+        load_c(1, 1)
+        load_v(1, 0)
+        load_b(2, 0, 2)
+        load_a(2)
+        load_c(2, 0)
+        load_c(2, 1)
+        load_v(1, 1)
+        load_v(2, 0)
+        load_v(2, 1)
+
+        def bank(kind):
+            bufs = {"ab": 3, "c": 3, "xt": 2}[kind]
+            return psum.tile([P, NT], F32, name=kind, tag=kind, bufs=bufs)
+
+        d_words = d_col[:].rearrange("p n t -> p (n t)").bitcast(F32)
+        d_row_words = d_row[:].rearrange("p n w -> p (n w)").bitcast(F32)
+        for n0, n1 in ((0, 2), (2, 3)):
+            xt = bank("xt")
+            for w in range(2 * n0, 2 * n1):
+                slot = w - 2 * n0
+                nc.tensor.transpose(
+                    xt[:, P * slot : P * (slot + 1)], d_words[:, w : w + 1].to_broadcast([P, P]), ident[:]
+                )
+            width = 2 * P * (n1 - n0)
+            nc.scalar.copy(
+                out=d_row_words[:, 2 * P * n0 : 2 * P * n1].rearrange("r (s p u) -> r s p u", p=P, u=2),
+                in_=xt[:, :width].rearrange("r (s u p) -> r s p u", p=P, u=2),
+            )
+
+        def f_operand(m, g):
+            k = [lo <= m < hi for lo, hi in F_CHUNKS].index(True)
+            off = (m - F_CHUNKS[k][0]) * P
+            return f_codes[k][:, g, off : off + P].bitcast(FP8X4), f_plane[:, g, P * m : P * (m + 1)]
+
+        def mm(acc, m, g, rhs, rhs_scale, start, stop):
+            lhs, lhs_scale = f_operand(m, g)
+            nc.tensor.matmul_mx(
+                out=acc[:], lhsT=lhs, lhsT_scale=lhs_scale, rhs=rhs, rhs_scale=rhs_scale, start=start, stop=stop
+            )
+
+        ab_acc, s_sb, y_bf, y_grp = {}, {}, {}, {}
+
+        def b_passes(i):
+            n, m = divmod(i, MTILES)
+            ab_acc[i] = bank("ab")
+            for g in range(PASSES):
+                mm(ab_acc[i], m, g, b_codes[n][:, g, :].bitcast(FP8X4), b_plane[4:P, g, NT * n : NT * (n + 1)], g == 0, False)
+
+        def a_passes(i):
+            n, m = divmod(i, MTILES)
+            for g in range(PASSES):
+                mm(ab_acc[i], m, g, a_codes[n][:, g, :].bitcast(FP4X4), a_plane[:, g, NT * n : NT * (n + 1)], False, g == PASSES - 1)
+
+        def scale_ab(i):
+            n, m = divmod(i, MTILES)
+            t = work.tile([P, NT], F32, name="t", tag="t", bufs=8)
+            nc.vector.tensor_tensor(out=t[:], in0=ab_acc[i][:], in1=d_row[:, n, :], op=MULT)
+            s_sb[i] = work.tile([P, NT], F32, name="s", tag="s", bufs=8)
+            nc.gpsimd.tensor_tensor(out=s_sb[i][:], in0=v_sb[n][m // V_HALF][:, m % V_HALF, :], in1=t[:], op=SUB)
+
+        def ab(i):
+            b_passes(i)
+            a_passes(i)
+            scale_ab(i)
+
+        def word_order(ap):
+            return ap.rearrange("r (p u e) -> r u p e", u=2, e=2)
+
+        def c_tile(j):
+            n, m = divmod(j, MTILES)
+            acc = bank("c")
+            for g in range(PASSES):
+                mm(acc, m, g, c_codes[n][g][:].bitcast(FP8X4), c_plane[n][g][:], g == 0, g == PASSES - 1)
+            y = work.tile([P, NT], F32, name="y", tag="y", bufs=12)
+            y_bf[j] = work.tile([P, 2, P, 2], BF16, name="y_bf", tag="y_bf", bufs=8, align_bytes=64)
+            if j == TILES - 1:
+                nc.vector.tensor_tensor(out=y_bf[j][:], in0=word_order(s_sb[j][:]), in1=word_order(acc[:]), op=SUB)
+            nc.vector.tensor_tensor(out=y[:], in0=s_sb[j][:], in1=acc[:], op=SUB)
+            nc.sync.dma_start(out=out_0[P * m : P * (m + 1), NT * n : NT * (n + 1)], in_=y[:])
+            if j < TILES - 1:
+                nc.scalar.copy(out=y_bf[j][:], in_=word_order(y[:]))
+
+        def interleave(engine_copy, n, g, h):
+            cols = slice(h * NT // 2, (h + 1) * NT // 2)
+            engine_copy(
+                out=c_grp[n][g][:, cols, :].rearrange("p (c i) t -> p c t i", i=4),
+                in_=c_raw[n][g][:, :, cols].rearrange("p t (c i) -> p c t i", i=4),
+            )
+
+        def quantize_c(n, g, lo, hi):
+            nc.vector.quantize_mx(
+                out=c_codes[n][g][:, lo:hi].bitcast(FP8X4),
+                scales=c_plane[n][g][:, lo:hi],
+                in_=c_grp[n][g][:, lo:hi, :].rearrange("p w t -> p (w t)"),
+            )
+
+        def turn(first, count, kind):
+            grp = work.tile([P, count * P, 4], BF16, name="y_grp", tag="y_grp", bufs=4, align_bytes=64)
+            y_grp[first] = grp
+            grp_words = grp[:].rearrange("p m t -> p (m t)").bitcast(F32)
+            banks = []
+            for lo in range(0, count, 2):
+                xt = bank(kind)
+                span = min(2, count - lo)
+                banks.append((xt, lo, span))
+                for s in range(span):
+                    words = y_bf[first + lo + s][:].rearrange("r u p e -> r (u p e)").bitcast(F32)
+                    for u in range(2):
+                        slot = 2 * s + u
+                        nc.tensor.transpose(xt[:, P * slot : P * (slot + 1)], words[:, P * u : P * (u + 1)], ident[:])
+            for xt, lo, span in banks:
+                nc.scalar.copy(
+                    out=grp_words[:, 2 * P * lo : 2 * P * (lo + span)].rearrange("p (s r u) -> p s r u", r=P, u=2),
+                    in_=xt[:, : 2 * P * span].rearrange("p (s u r) -> p s r u", r=P, u=2),
+                )
+
+        def quantize_y(first, count):
+            n, m = divmod(first, MTILES)
+            cols = slice(P * m, P * (m + count))
+            nc.vector.quantize_mx(
+                out=y_codes[n][:, cols].bitcast(FP8X4),
+                scales=y_plane[n][:, cols],
+                in_=y_grp[first][:].rearrange("p m t -> p (m t)"),
+            )
+            nc.sync.dma_start(
+                out=out_1[n].rearrange("p m t -> p (m t)")[:, 4 * P * m : 4 * P * (m + count)].bitcast(I32),
+                in_=y_codes[n][:, cols].bitcast(I32),
+            )
+            if m + count == MTILES:
+                for q in range(4):
+                    nc.sync.dma_start(
+                        out=out_2[n, 4 * q : 4 * q + 4, :].bitcast(I32),
+                        in_=y_plane[n][32 * q : 32 * q + 4, :].bitcast(I32),
+                    )
+
+        half = NT // 2
+        b_passes(0)
+        b_passes(1)
+        a_passes(0)
+        scale_ab(0)
+        a_passes(1)
+        scale_ab(1)
+        interleave(nc.scalar.copy, 0, 0, 1)
+        interleave(nc.scalar.copy, 0, 1, 1)
+        interleave(nc.vector.tensor_copy, 0, 0, 0)
+        ab(2)
+        interleave(nc.vector.tensor_copy, 0, 1, 0)
+        quantize_c(0, 0, 0, NT)
+        ab(3)
+        quantize_c(0, 1, 0, NT)
+        ab(4)
+        ab(5)
+
+        ab_after = {j: j + LEAD for j in range(15)}
+        ab_after.update({16: 21, 18: 22, 20: 23})
+        for j in range(TILES):
+            n, m = divmod(j, MTILES)
+            c_tile(j)
+            if n + 1 < NTILES and 1 <= m <= 4:
+                g, h = divmod(m - 1, 2)
+                interleave(nc.scalar.copy, n + 1, g, h)
+            if j in ab_after:
+                ab(ab_after[j])
+            if n + 1 < NTILES and m in (3, 5):
+                quantize_c(n + 1, (m - 3) // 2, 0, NT)
+            if j >= 4 and j % 4 == 0:
+                turn(j - 4, 4, "xt")
+            if j >= 6 and j % 4 == 2 and j < 20:
+                quantize_y(j - 6, 4)
+        turn(20, 2, "ab")
+        turn(22, 1, "ab")
+        turn(23, 1, "ab")
+        quantize_y(16, 4)
+        quantize_y(20, 2)
+        quantize_y(22, 1)
+        quantize_y(23, 1)

@@ -22,9 +22,9 @@ PASSES = BLK // 512
 MTILES = ROWS // P
 NTILES = REST // NT
 TILES = MTILES * NTILES
-LEAD = 6
+LEAD = 7
+WARM = 5
 F_CHUNKS = [(0, 2), (2, 4), (4, 8)]
-V_HALF = 4
 
 
 def tile_lazy_pruning_update_k3_kernel(
@@ -50,7 +50,7 @@ def tile_lazy_pruning_update_k3_kernel(
         c_grp = [[kept("c_grp%d_%d" % (n, g), [P, NT, 4], BF16) for g in range(PASSES)] for n in range(NTILES)]
         c_codes = [[kept("c_codes%d_%d" % (n, g), [P, NT], U32) for g in range(PASSES)] for n in range(NTILES)]
         c_plane = [[kept("c_plane%d_%d" % (n, g), [P, NT], U8) for g in range(PASSES)] for n in range(NTILES)]
-        v_sb = [[kept("v%d_%d" % (n, h), [P, V_HALF, NT], BF16) for h in range(2)] for n in range(NTILES)]
+        v_sb = [kept("v%d" % n, [P, MTILES, NT], BF16) for n in range(NTILES)]
         d_col = kept("d_col", [P, NTILES, 4], BF16)
         d_row = kept("d_row", [P, NTILES, NT], BF16)
         ident = kept("ident", [P, P], F32)
@@ -86,14 +86,14 @@ def tile_lazy_pruning_update_k3_kernel(
             rows = c[512 * g : 512 * (g + 1), NT * n : NT * (n + 1)]
             nc.sync.dma_start(out=c_raw[n][g][:], in_=rows.rearrange("(p j) w -> p j w", j=4))
 
-        def load_v(n, h):
-            rows = v[V_HALF * P * h : V_HALF * P * (h + 1), NT * n : NT * (n + 1)]
-            nc.sync.dma_start(out=v_sb[n][h][:], in_=rows.rearrange("(m p) w -> p m w", p=P))
+        def load_v(n, lo, hi):
+            rows = v[P * lo : P * hi, NT * n : NT * (n + 1)]
+            nc.sync.dma_start(out=v_sb[n][:, lo:hi, :], in_=rows.rearrange("(m p) w -> p m w", p=P))
 
         nc.gpsimd.dma_start(out=d_col[:], in_=d.rearrange("(n p t) -> p n t", p=P, t=4))
+        make_identity(nc, ident[:])
         for plane in (f_plane, b_plane, a_plane):
             nc.vector.memset(plane[:].rearrange("p g n -> p (g n)").bitcast(I32), 0)
-        make_identity(nc, ident[:])
 
         load_f(0)
         load_b(0, 0, 1)
@@ -103,23 +103,24 @@ def tile_lazy_pruning_update_k3_kernel(
         load_a(0)
         load_scales(nc.sync, a_plane, a_scales, 0)
         load_f(1)
+        load_v(0, 0, 2)
         load_c(0, 0)
         load_c(0, 1)
+        load_v(0, 2, 4)
         load_f(2)
+        load_v(0, 4, 8)
         load_b(1, 0, 2)
         load_a(1)
-        load_v(0, 0)
         load_c(1, 0)
-        load_v(0, 1)
         load_c(1, 1)
-        load_v(1, 0)
+        load_v(1, 0, 4)
+        load_v(1, 4, 8)
         load_b(2, 0, 2)
         load_a(2)
         load_c(2, 0)
         load_c(2, 1)
-        load_v(1, 1)
-        load_v(2, 0)
-        load_v(2, 1)
+        load_v(2, 0, 4)
+        load_v(2, 4, 8)
 
         def bank(kind):
             bufs = {"ab": 3, "c": 3, "xt": 2}[kind]
@@ -127,7 +128,8 @@ def tile_lazy_pruning_update_k3_kernel(
 
         d_words = d_col[:].rearrange("p n t -> p (n t)").bitcast(F32)
         d_row_words = d_row[:].rearrange("p n w -> p (n w)").bitcast(F32)
-        for n0, n1 in ((0, 2), (2, 3)):
+
+        def spread_d(n0, n1):
             xt = bank("xt")
             for w in range(2 * n0, 2 * n1):
                 slot = w - 2 * n0
@@ -151,7 +153,7 @@ def tile_lazy_pruning_update_k3_kernel(
                 out=acc[:], lhsT=lhs, lhsT_scale=lhs_scale, rhs=rhs, rhs_scale=rhs_scale, start=start, stop=stop
             )
 
-        ab_acc, s_sb, y_bf, y_grp = {}, {}, {}, {}
+        ab_acc, t_sb, s_sb, y_bf, y_grp = {}, {}, {}, {}, {}
 
         def b_passes(i):
             n, m = divmod(i, MTILES)
@@ -165,11 +167,14 @@ def tile_lazy_pruning_update_k3_kernel(
                 mm(ab_acc[i], m, g, a_codes[n][:, g, :].bitcast(FP4X4), a_plane[:, g, NT * n : NT * (n + 1)], False, g == PASSES - 1)
 
         def scale_ab(i):
+            n = i // MTILES
+            t_sb[i] = work.tile([P, NT], F32, name="t", tag="t", bufs=3)
+            nc.vector.tensor_tensor(out=t_sb[i][:], in0=ab_acc[i][:], in1=d_row[:, n, :], op=MULT)
+
+        def subtract_from_v(i):
             n, m = divmod(i, MTILES)
-            t = work.tile([P, NT], F32, name="t", tag="t", bufs=8)
-            nc.vector.tensor_tensor(out=t[:], in0=ab_acc[i][:], in1=d_row[:, n, :], op=MULT)
-            s_sb[i] = work.tile([P, NT], F32, name="s", tag="s", bufs=8)
-            nc.gpsimd.tensor_tensor(out=s_sb[i][:], in0=v_sb[n][m // V_HALF][:, m % V_HALF, :], in1=t[:], op=SUB)
+            s_sb[i] = work.tile([P, NT], F32, name="s", tag="s", bufs=9)
+            nc.vector.tensor_tensor(out=s_sb[i][:], in0=v_sb[n][:, m, :], in1=t_sb[i][:], op=SUB)
 
         def ab(i):
             b_passes(i)
@@ -246,34 +251,45 @@ def tile_lazy_pruning_update_k3_kernel(
                         in_=y_plane[n][32 * q : 32 * q + 4, :].bitcast(I32),
                     )
 
-        half = NT // 2
+        warm = bank("c")
+        for k in range(WARM):
+            lhs, lhs_scale = f_operand(0, 0)
+            nc.tensor.matmul_mx(
+                out=warm[:, : 2 * P], lhsT=lhs, lhsT_scale=lhs_scale, rhs=f_codes[0][:, 0, :].bitcast(FP8X4),
+                rhs_scale=f_plane[:, 0, : 2 * P], start=True, stop=True,
+            )
+        spread_d(0, 1)
+        for g in range(PASSES):
+            for h in range(2):
+                interleave(nc.scalar.copy, 0, g, h)
         b_passes(0)
         b_passes(1)
         a_passes(0)
         scale_ab(0)
         a_passes(1)
         scale_ab(1)
-        interleave(nc.scalar.copy, 0, 0, 1)
-        interleave(nc.scalar.copy, 0, 1, 1)
-        interleave(nc.vector.tensor_copy, 0, 0, 0)
-        ab(2)
-        interleave(nc.vector.tensor_copy, 0, 1, 0)
-        quantize_c(0, 0, 0, NT)
-        ab(3)
-        quantize_c(0, 1, 0, NT)
-        ab(4)
-        ab(5)
+        for i in range(2, LEAD):
+            subtract_from_v(i - 2)
+            ab(i)
+            if i in (3, 5):
+                quantize_c(0, (i - 3) // 2, 0, NT)
+        subtract_from_v(LEAD - 2)
+        spread_d(1, 3)
 
-        ab_after = {j: j + LEAD for j in range(15)}
+        ab_after = {j: j + LEAD for j in range(14)}
         ab_after.update({16: 21, 18: 22, 20: 23})
+        pending = LEAD - 1
         for j in range(TILES):
             n, m = divmod(j, MTILES)
             c_tile(j)
+            if pending is not None:
+                subtract_from_v(pending)
+            pending = ab_after.get(j)
             if n + 1 < NTILES and 1 <= m <= 4:
                 g, h = divmod(m - 1, 2)
                 interleave(nc.scalar.copy, n + 1, g, h)
-            if j in ab_after:
-                ab(ab_after[j])
+            if pending is not None:
+                ab(pending)
             if n + 1 < NTILES and m in (3, 5):
                 quantize_c(n + 1, (m - 3) // 2, 0, NT)
             if j >= 4 and j % 4 == 0:

@@ -22,9 +22,11 @@ PASSES = BLK // 512
 MTILES = ROWS // P
 NTILES = REST // NT
 TILES = MTILES * NTILES
-LEAD = 7
+LEAD = 8
 WARM = 5
-F_CHUNKS = [(0, 2), (2, 4), (4, 8)]
+S_BUFS = 3
+SKIP = (6, 14, 16, 18)
+F_CHUNKS = [(0, 2), (2, 4), (4, 6), (6, 8)]
 
 
 def tile_lazy_pruning_update_k3_kernel(
@@ -41,8 +43,9 @@ def tile_lazy_pruning_update_k3_kernel(
             return keep.tile(shape, dtype, name=name, align_bytes=64)
 
         f_plane = kept("f_plane", [P, PASSES, ROWS], U8)
-        a_plane = kept("a_plane", [P, PASSES, REST], U8)
-        b_plane = kept("b_plane", [P, PASSES, REST], U8)
+        a_first = kept("a_first", [P, PASSES, NT], U8)
+        b_first = kept("b_first", [P, PASSES, NT], U8)
+        ab_rest = kept("ab_rest", [P, PASSES, REST - NT], U8)
         f_codes = [kept("f_codes%d" % lo, [P, PASSES, (hi - lo) * P], U32) for lo, hi in F_CHUNKS]
         a_codes = [kept("a_codes%d" % n, [P, PASSES, 2 * NT], U8) for n in range(NTILES)]
         b_codes = [kept("b_codes%d" % n, [P, PASSES, NT], U32) for n in range(NTILES)]
@@ -73,11 +76,11 @@ def tile_lazy_pruning_update_k3_kernel(
             lo, hi = F_CHUNKS[k]
             nc.sync.dma_start(out=f_codes[k][:].bitcast(I32), in_=f_view[:, :, 4 * P * lo : 4 * P * hi].bitcast(I32))
 
-        def load_a(n):
-            nc.sync.dma_start(out=a_codes[n][:].bitcast(I32), in_=a_view[:, :, 2 * NT * n : 2 * NT * (n + 1)].bitcast(I32))
+        def load_a(queue, n):
+            queue.dma_start(out=a_codes[n][:].bitcast(I32), in_=a_view[:, :, 2 * NT * n : 2 * NT * (n + 1)].bitcast(I32))
 
-        def load_b(n, g0, g1):
-            nc.sync.dma_start(
+        def load_b(queue, n, g0, g1):
+            queue.dma_start(
                 out=b_codes[n][:, g0:g1, :].bitcast(I32),
                 in_=b_view[:, g0:g1, 4 * NT * n : 4 * NT * (n + 1)].bitcast(I32),
             )
@@ -90,35 +93,38 @@ def tile_lazy_pruning_update_k3_kernel(
             rows = v[P * lo : P * hi, NT * n : NT * (n + 1)]
             nc.sync.dma_start(out=v_sb[n][:, lo:hi, :], in_=rows.rearrange("(m p) w -> p m w", p=P))
 
-        nc.gpsimd.dma_start(out=d_col[:], in_=d.rearrange("(n p t) -> p n t", p=P, t=4))
+        nc.sync.dma_start(out=d_col[:], in_=d.rearrange("(n p t) -> p n t", p=P, t=4))
+        load_b(nc.gpsimd, 0, 0, 1)
+        load_a(nc.gpsimd, 0)
         make_identity(nc, ident[:])
-        for plane in (f_plane, b_plane, a_plane):
+        for plane in (f_plane, b_first, a_first, ab_rest):
             nc.vector.memset(plane[:].rearrange("p g n -> p (g n)").bitcast(I32), 0)
 
         load_f(0)
-        load_b(0, 0, 1)
         load_scales(nc.sync, f_plane, f_scales, 0)
-        load_scales(nc.sync, b_plane, b_scales, 4)
-        load_b(0, 1, 2)
-        load_a(0)
-        load_scales(nc.sync, a_plane, a_scales, 0)
+        load_scales(nc.sync, b_first, b_scales[:, :, :NT], 4)
+        load_b(nc.sync, 0, 1, 2)
+        load_scales(nc.sync, a_first, a_scales[:, :, :NT], 0)
         load_f(1)
-        load_v(0, 0, 2)
-        load_c(0, 0)
-        load_c(0, 1)
-        load_v(0, 2, 4)
         load_f(2)
-        load_v(0, 4, 8)
-        load_b(1, 0, 2)
-        load_a(1)
+        load_c(0, 0)
+        load_f(3)
+        load_c(0, 1)
+        load_scales(nc.sync, ab_rest, b_scales[:, :, NT:], 4)
+        load_scales(nc.sync, ab_rest, a_scales[:, :, NT:], 0)
+        load_v(0, 0, 2)
+        load_b(nc.sync, 1, 0, 2)
+        load_a(nc.sync, 1)
+        load_v(0, 2, 4)
         load_c(1, 0)
+        load_v(0, 4, 8)
         load_c(1, 1)
         load_v(1, 0, 4)
-        load_v(1, 4, 8)
-        load_b(2, 0, 2)
-        load_a(2)
+        load_b(nc.sync, 2, 0, 2)
+        load_a(nc.sync, 2)
         load_c(2, 0)
         load_c(2, 1)
+        load_v(1, 4, 8)
         load_v(2, 0, 4)
         load_v(2, 4, 8)
 
@@ -155,26 +161,33 @@ def tile_lazy_pruning_update_k3_kernel(
 
         ab_acc, t_sb, s_sb, y_bf, y_grp = {}, {}, {}, {}, {}
 
-        def b_passes(i):
+        def plane_of(first, n, g, row):
+            if n == 0:
+                return first[row:P, g, :]
+            return ab_rest[row:P, g, NT * (n - 1) : NT * n]
+
+        def b_passes(i, passes=range(PASSES)):
             n, m = divmod(i, MTILES)
-            ab_acc[i] = bank("ab")
-            for g in range(PASSES):
-                mm(ab_acc[i], m, g, b_codes[n][:, g, :].bitcast(FP8X4), b_plane[4:P, g, NT * n : NT * (n + 1)], g == 0, False)
+            for g in passes:
+                if g == 0:
+                    ab_acc[i] = bank("ab")
+                mm(ab_acc[i], m, g, b_codes[n][:, g, :].bitcast(FP8X4), plane_of(b_first, n, g, 4), g == 0, False)
 
         def a_passes(i):
             n, m = divmod(i, MTILES)
             for g in range(PASSES):
-                mm(ab_acc[i], m, g, a_codes[n][:, g, :].bitcast(FP4X4), a_plane[:, g, NT * n : NT * (n + 1)], False, g == PASSES - 1)
+                mm(ab_acc[i], m, g, a_codes[n][:, g, :].bitcast(FP4X4), plane_of(a_first, n, g, 0), False, g == PASSES - 1)
 
         def scale_ab(i):
             n = i // MTILES
-            t_sb[i] = work.tile([P, NT], F32, name="t", tag="t", bufs=3)
-            nc.vector.tensor_tensor(out=t_sb[i][:], in0=ab_acc[i][:], in1=d_row[:, n, :], op=MULT)
+            t_sb[i] = work.tile([P, NT], F32, name="t", tag="t", bufs=9)
+            nc.vector.tensor_tensor(out=t_sb[i][:], in0=d_row[:, n, :], in1=ab_acc[i][:], op=MULT)
 
         def subtract_from_v(i):
             n, m = divmod(i, MTILES)
-            s_sb[i] = work.tile([P, NT], F32, name="s", tag="s", bufs=9)
-            nc.vector.tensor_tensor(out=s_sb[i][:], in0=v_sb[n][:, m, :], in1=t_sb[i][:], op=SUB)
+            tag = "s" if i < TILES - 1 else "s_last"
+            s_sb[i] = work.tile([P, NT], F32, name=tag, tag=tag, bufs=3)
+            nc.gpsimd.tensor_tensor(out=s_sb[i][:], in0=v_sb[n][:, m, :], in1=t_sb[i][:], op=SUB)
 
         def ab(i):
             b_passes(i)
@@ -258,44 +271,45 @@ def tile_lazy_pruning_update_k3_kernel(
                 out=warm[:, : 2 * P], lhsT=lhs, lhsT_scale=lhs_scale, rhs=f_codes[0][:, 0, :].bitcast(FP8X4),
                 rhs_scale=f_plane[:, 0, : 2 * P], start=True, stop=True,
             )
-        spread_d(0, 1)
+        b_passes(0, [0])
+        b_passes(1, [0])
+        spread_d(0, 2)
+        spread_d(2, 3)
         for g in range(PASSES):
-            for h in range(2):
-                interleave(nc.scalar.copy, 0, g, h)
-        b_passes(0)
-        b_passes(1)
+            interleave(nc.scalar.copy, 0, g, 1)
+        b_passes(0, [1])
+        b_passes(1, [1])
         a_passes(0)
         scale_ab(0)
         a_passes(1)
         scale_ab(1)
         for i in range(2, LEAD):
-            subtract_from_v(i - 2)
             ab(i)
+            if i in (2, 4):
+                interleave(nc.vector.tensor_copy, 0, (i - 2) // 2, 0)
             if i in (3, 5):
                 quantize_c(0, (i - 3) // 2, 0, NT)
-        subtract_from_v(LEAD - 2)
-        spread_d(1, 3)
+        for i in range(S_BUFS):
+            subtract_from_v(i)
 
-        ab_after = {j: j + LEAD for j in range(14)}
-        ab_after.update({16: 21, 18: 22, 20: 23})
-        pending = LEAD - 1
+        next_ab = LEAD
         for j in range(TILES):
             n, m = divmod(j, MTILES)
             c_tile(j)
-            if pending is not None:
-                subtract_from_v(pending)
-            pending = ab_after.get(j)
+            if n + 1 < NTILES and m in (4, 6):
+                quantize_c(n + 1, (m - 4) // 2, 0, NT)
+            if j >= 6 and j % 4 == 2 and j < 20:
+                quantize_y(j - 6, 4)
             if n + 1 < NTILES and 1 <= m <= 4:
                 g, h = divmod(m - 1, 2)
                 interleave(nc.scalar.copy, n + 1, g, h)
-            if pending is not None:
-                ab(pending)
-            if n + 1 < NTILES and m in (3, 5):
-                quantize_c(n + 1, (m - 3) // 2, 0, NT)
+            if j not in SKIP and next_ab < TILES:
+                ab(next_ab)
+                next_ab += 1
+            if j + S_BUFS < TILES:
+                subtract_from_v(j + S_BUFS)
             if j >= 4 and j % 4 == 0:
                 turn(j - 4, 4, "xt")
-            if j >= 6 and j % 4 == 2 and j < 20:
-                quantize_y(j - 6, 4)
         turn(20, 2, "ab")
         turn(22, 1, "ab")
         turn(23, 1, "ab")

@@ -22,10 +22,10 @@ PASSES = BLK // 512
 MTILES = ROWS // P
 NTILES = REST // NT
 TILES = MTILES * NTILES
-LEAD = 8
+LEAD_FIRST = 8
 WARM = 5
 S_BUFS = 3
-SKIP = (6, 14, 16, 18)
+GROUP = 4
 F_CHUNKS = [(0, 2), (2, 4), (4, 6), (6, 8)]
 
 
@@ -183,11 +183,11 @@ def tile_lazy_pruning_update_k3_kernel(
             t_sb[i] = work.tile([P, NT], F32, name="t", tag="t", bufs=9)
             nc.vector.tensor_tensor(out=t_sb[i][:], in0=d_row[:, n, :], in1=ab_acc[i][:], op=MULT)
 
-        def subtract_from_v(i):
+        def subtract_from_v(engine, i):
             n, m = divmod(i, MTILES)
-            tag = "s" if i < TILES - 1 else "s_last"
-            s_sb[i] = work.tile([P, NT], F32, name=tag, tag=tag, bufs=3)
-            nc.gpsimd.tensor_tensor(out=s_sb[i][:], in0=v_sb[n][:, m, :], in1=t_sb[i][:], op=SUB)
+            tag, bufs = ("s", S_BUFS) if i < TILES - 1 else ("s_last", 1)
+            s_sb[i] = work.tile([P, NT], F32, name=tag, tag=tag, bufs=bufs)
+            engine.tensor_tensor(out=s_sb[i][:], in0=v_sb[n][:, m, :], in1=t_sb[i][:], op=SUB)
 
         def ab(i):
             b_passes(i)
@@ -218,15 +218,15 @@ def tile_lazy_pruning_update_k3_kernel(
                 in_=c_raw[n][g][:, :, cols].rearrange("p t (c i) -> p c t i", i=4),
             )
 
-        def quantize_c(n, g, lo, hi):
+        def quantize_c(n, g):
             nc.vector.quantize_mx(
-                out=c_codes[n][g][:, lo:hi].bitcast(FP8X4),
-                scales=c_plane[n][g][:, lo:hi],
-                in_=c_grp[n][g][:, lo:hi, :].rearrange("p w t -> p (w t)"),
+                out=c_codes[n][g][:].bitcast(FP8X4),
+                scales=c_plane[n][g][:],
+                in_=c_grp[n][g][:].rearrange("p w t -> p (w t)"),
             )
 
         def turn(first, count, kind):
-            grp = work.tile([P, count * P, 4], BF16, name="y_grp", tag="y_grp", bufs=4, align_bytes=64)
+            grp = work.tile([P, count * P, 4], BF16, name="y_grp", tag="y_grp", bufs=5, align_bytes=64)
             y_grp[first] = grp
             grp_words = grp[:].rearrange("p m t -> p (m t)").bitcast(F32)
             banks = []
@@ -253,6 +253,10 @@ def tile_lazy_pruning_update_k3_kernel(
                 scales=y_plane[n][:, cols],
                 in_=y_grp[first][:].rearrange("p m t -> p (m t)"),
             )
+
+        def store_planes(first, count):
+            n, m = divmod(first, MTILES)
+            cols = slice(P * m, P * (m + count))
             nc.sync.dma_start(
                 out=out_1[n].rearrange("p m t -> p (m t)")[:, 4 * P * m : 4 * P * (m + count)].bitcast(I32),
                 in_=y_codes[n][:, cols].bitcast(I32),
@@ -283,37 +287,51 @@ def tile_lazy_pruning_update_k3_kernel(
         scale_ab(0)
         a_passes(1)
         scale_ab(1)
-        for i in range(2, LEAD):
+        for i in range(2, LEAD_FIRST):
             ab(i)
             if i in (2, 4):
                 interleave(nc.vector.tensor_copy, 0, (i - 2) // 2, 0)
             if i in (3, 5):
-                quantize_c(0, (i - 3) // 2, 0, NT)
+                quantize_c(0, (i - 3) // 2)
         for i in range(S_BUFS):
-            subtract_from_v(i)
+            subtract_from_v(nc.gpsimd, i)
 
-        next_ab = LEAD
-        for j in range(TILES):
+        next_ab = LEAD_FIRST
+        last_group = TILES - GROUP
+        for j in range(last_group):
             n, m = divmod(j, MTILES)
-            c_tile(j)
-            if n + 1 < NTILES and m in (4, 6):
-                quantize_c(n + 1, (m - 4) // 2, 0, NT)
-            if j >= 6 and j % 4 == 2 and j < 20:
-                quantize_y(j - 6, 4)
             if n + 1 < NTILES and 1 <= m <= 4:
                 g, h = divmod(m - 1, 2)
                 interleave(nc.scalar.copy, n + 1, g, h)
-            if j not in SKIP and next_ab < TILES:
+            c_tile(j)
+            turning = j > GROUP and j % GROUP == 1
+            if n + 1 < NTILES and m in (4, 6):
+                quantize_c(n + 1, (m - 4) // 2)
+            if j > GROUP and j % GROUP == 3:
+                quantize_y(j - 7, GROUP)
+                store_planes(j - 7, GROUP)
+            if turning:
+                subtract_from_v(nc.vector, j + S_BUFS)
+                turn(j - 5, GROUP, "xt")
+            else:
                 ab(next_ab)
                 next_ab += 1
-            if j + S_BUFS < TILES:
-                subtract_from_v(j + S_BUFS)
-            if j >= 4 and j % 4 == 0:
-                turn(j - 4, 4, "xt")
+                subtract_from_v(nc.gpsimd, j + S_BUFS)
+        subtract_from_v(nc.gpsimd, TILES - 1)
+        turn(16, 2, "xt")
+        c_tile(20)
+        c_tile(21)
+        turn(18, 2, "xt")
+        quantize_y(16, 2)
+        c_tile(22)
+        c_tile(23)
         turn(20, 2, "ab")
         turn(22, 1, "ab")
         turn(23, 1, "ab")
-        quantize_y(16, 4)
+        quantize_y(18, 2)
+        store_planes(16, 4)
         quantize_y(20, 2)
         quantize_y(22, 1)
+        store_planes(20, 3)
         quantize_y(23, 1)
+        store_planes(23, 1)

@@ -23,10 +23,11 @@ MTILES = ROWS // P
 NTILES = REST // NT
 TILES = MTILES * NTILES
 LEAD_FIRST = 8
-WARM = 5
+WARM = 3
 S_BUFS = 3
 GROUP = 4
-F_CHUNKS = [(0, 2), (2, 4), (4, 6), (6, 8)]
+F_CHUNKS = [(0, 2), (2, 5), (5, 8)]
+HEAD_TILES = F_CHUNKS[0][1]
 
 
 def tile_lazy_pruning_update_k3_kernel(
@@ -46,15 +47,18 @@ def tile_lazy_pruning_update_k3_kernel(
         a_first = kept("a_first", [P, PASSES, NT], U8)
         b_first = kept("b_first", [P, PASSES, NT], U8)
         ab_rest = kept("ab_rest", [P, PASSES, REST - NT], U8)
-        f_codes = [kept("f_codes%d" % lo, [P, PASSES, (hi - lo) * P], U32) for lo, hi in F_CHUNKS]
+        f_head = [kept("f_head%d" % g, [P, HEAD_TILES * P], U32) for g in range(PASSES)]
+        f_codes = [kept("f_codes%d" % lo, [P, PASSES, (hi - lo) * P], U32) if lo else None for lo, hi in F_CHUNKS]
         a_codes = [kept("a_codes%d" % n, [P, PASSES, 2 * NT], U8) for n in range(NTILES)]
         b_codes = [kept("b_codes%d" % n, [P, PASSES, NT], U32) for n in range(NTILES)]
         c_raw = [[kept("c_raw%d_%d" % (n, g), [P, 4, NT], BF16) for g in range(PASSES)] for n in range(NTILES)]
-        c_grp = [[kept("c_grp%d_%d" % (n, g), [P, NT, 4], BF16) for g in range(PASSES)] for n in range(NTILES)]
+        c_grp = [[kept("c_grp%d_%d" % (n, g), [P, NT, 4], BF16) if (n, g) != (0, 1) else None for g in range(PASSES)]
+                 for n in range(NTILES)]
+        c_grp[0][1] = work.tile([P, NT, 4], BF16, name="c_grp0_1", tag="shared", bufs=1, align_bytes=64)
         c_codes = [[kept("c_codes%d_%d" % (n, g), [P, NT], U32) for g in range(PASSES)] for n in range(NTILES)]
         c_plane = [[kept("c_plane%d_%d" % (n, g), [P, NT], U8) for g in range(PASSES)] for n in range(NTILES)]
         v_sb = [kept("v%d" % n, [P, MTILES, NT], BF16) for n in range(NTILES)]
-        d_col = kept("d_col", [P, NTILES, 4], BF16)
+        d_col = kept("d_col", [P, REST // P], BF16)
         d_row = kept("d_row", [P, NTILES, NT], BF16)
         ident = kept("ident", [P, P], F32)
         y_codes = [kept("y_codes%d" % n, [P, ROWS], U32) for n in range(NTILES)]
@@ -76,6 +80,9 @@ def tile_lazy_pruning_update_k3_kernel(
             lo, hi = F_CHUNKS[k]
             nc.sync.dma_start(out=f_codes[k][:].bitcast(I32), in_=f_view[:, :, 4 * P * lo : 4 * P * hi].bitcast(I32))
 
+        def load_f_head(g):
+            nc.sync.dma_start(out=f_head[g][:].bitcast(I32), in_=f_view[:, g, : 4 * P * HEAD_TILES].bitcast(I32))
+
         def load_a(queue, n):
             queue.dma_start(out=a_codes[n][:].bitcast(I32), in_=a_view[:, :, 2 * NT * n : 2 * NT * (n + 1)].bitcast(I32))
 
@@ -93,22 +100,21 @@ def tile_lazy_pruning_update_k3_kernel(
             rows = v[P * lo : P * hi, NT * n : NT * (n + 1)]
             nc.sync.dma_start(out=v_sb[n][:, lo:hi, :], in_=rows.rearrange("(m p) w -> p m w", p=P))
 
-        nc.sync.dma_start(out=d_col[:], in_=d.rearrange("(n p t) -> p n t", p=P, t=4))
         load_b(nc.gpsimd, 0, 0, 1)
-        load_a(nc.gpsimd, 0)
         make_identity(nc, ident[:])
         for plane in (f_plane, b_first, a_first, ab_rest):
             nc.vector.memset(plane[:].rearrange("p g n -> p (g n)").bitcast(I32), 0)
-
-        load_f(0)
+        nc.sync.dma_start(out=d_col[:], in_=d.rearrange("(p j) -> p j", p=P))
+        load_f_head(0)
         load_scales(nc.sync, f_plane, f_scales, 0)
         load_scales(nc.sync, b_first, b_scales[:, :, :NT], 4)
+        load_f_head(1)
         load_b(nc.sync, 0, 1, 2)
+        load_a(nc.sync, 0)
         load_scales(nc.sync, a_first, a_scales[:, :, :NT], 0)
         load_f(1)
-        load_f(2)
         load_c(0, 0)
-        load_f(3)
+        load_f(2)
         load_c(0, 1)
         load_scales(nc.sync, ab_rest, b_scales[:, :, NT:], 4)
         load_scales(nc.sync, ab_rest, a_scales[:, :, NT:], 0)
@@ -132,26 +138,23 @@ def tile_lazy_pruning_update_k3_kernel(
             bufs = {"ab": 3, "c": 3, "xt": 2}[kind]
             return psum.tile([P, NT], F32, name=kind, tag=kind, bufs=bufs)
 
-        d_words = d_col[:].rearrange("p n t -> p (n t)").bitcast(F32)
-        d_row_words = d_row[:].rearrange("p n w -> p (n w)").bitcast(F32)
+        d_words = d_col[:].bitcast(F32)
+        d_row_words = d_row[:].rearrange("r n w -> r (n w)").bitcast(F32).rearrange("r (p w) -> r p w", p=P)
 
-        def spread_d(n0, n1):
+        def spread_d(w0, w1):
             xt = bank("xt")
-            for w in range(2 * n0, 2 * n1):
-                slot = w - 2 * n0
+            for w in range(w0, w1):
+                slot = w - w0
                 nc.tensor.transpose(
                     xt[:, P * slot : P * (slot + 1)], d_words[:, w : w + 1].to_broadcast([P, P]), ident[:]
                 )
-            width = 2 * P * (n1 - n0)
-            nc.scalar.copy(
-                out=d_row_words[:, 2 * P * n0 : 2 * P * n1].rearrange("r (s p u) -> r s p u", p=P, u=2),
-                in_=xt[:, :width].rearrange("r (s u p) -> r s p u", p=P, u=2),
-            )
+            nc.scalar.copy(out=d_row_words[:, :, w0:w1], in_=xt[:, : P * (w1 - w0)].rearrange("r (w p) -> r p w", p=P))
 
         def f_operand(m, g):
             k = [lo <= m < hi for lo, hi in F_CHUNKS].index(True)
             off = (m - F_CHUNKS[k][0]) * P
-            return f_codes[k][:, g, off : off + P].bitcast(FP8X4), f_plane[:, g, P * m : P * (m + 1)]
+            codes = f_codes[k][:, g, off : off + P] if k else f_head[g][:, off : off + P]
+            return codes.bitcast(FP8X4), f_plane[:, g, P * m : P * (m + 1)]
 
         def mm(acc, m, g, rhs, rhs_scale, start, stop):
             lhs, lhs_scale = f_operand(m, g)
@@ -185,8 +188,8 @@ def tile_lazy_pruning_update_k3_kernel(
 
         def subtract_from_v(engine, i):
             n, m = divmod(i, MTILES)
-            tag, bufs = ("s", S_BUFS) if i < TILES - 1 else ("s_last", 1)
-            s_sb[i] = work.tile([P, NT], F32, name=tag, tag=tag, bufs=bufs)
+            tag, bufs = {0: ("shared", 1), TILES - 1: ("s_last", 1)}.get(i, ("s", S_BUFS))
+            s_sb[i] = work.tile([P, NT], F32, name=tag, tag=tag, bufs=bufs, align_bytes=64)
             engine.tensor_tensor(out=s_sb[i][:], in0=v_sb[n][:, m, :], in1=t_sb[i][:], op=SUB)
 
         def ab(i):
@@ -268,31 +271,29 @@ def tile_lazy_pruning_update_k3_kernel(
                         in_=y_plane[n][32 * q : 32 * q + 4, :].bitcast(I32),
                     )
 
+        spread_d(0, 4)
+        spread_d(4, 6)
         warm = bank("c")
         for k in range(WARM):
             lhs, lhs_scale = f_operand(0, 0)
             nc.tensor.matmul_mx(
-                out=warm[:, : 2 * P], lhsT=lhs, lhsT_scale=lhs_scale, rhs=f_codes[0][:, 0, :].bitcast(FP8X4),
+                out=warm[:, : 2 * P], lhsT=lhs, lhsT_scale=lhs_scale, rhs=f_head[0][:, : 2 * P].bitcast(FP8X4),
                 rhs_scale=f_plane[:, 0, : 2 * P], start=True, stop=True,
             )
-        b_passes(0, [0])
-        b_passes(1, [0])
-        spread_d(0, 2)
-        spread_d(2, 3)
+        for g in range(PASSES):
+            for i in range(HEAD_TILES):
+                b_passes(i, [g])
         for g in range(PASSES):
             interleave(nc.scalar.copy, 0, g, 1)
-        b_passes(0, [1])
-        b_passes(1, [1])
-        a_passes(0)
-        scale_ab(0)
-        a_passes(1)
-        scale_ab(1)
-        for i in range(2, LEAD_FIRST):
+        for i in range(HEAD_TILES):
+            a_passes(i)
+            scale_ab(i)
+        for i in range(HEAD_TILES, LEAD_FIRST):
             ab(i)
             if i in (2, 4):
-                interleave(nc.vector.tensor_copy, 0, (i - 2) // 2, 0)
+                interleave(nc.vector.tensor_copy, 0, (2, 4).index(i), 0)
             if i in (3, 5):
-                quantize_c(0, (i - 3) // 2)
+                quantize_c(0, (3, 5).index(i))
         for i in range(S_BUFS):
             subtract_from_v(nc.gpsimd, i)
 

@@ -18,12 +18,14 @@ SUB = mybir.AluOpType.subtract
 
 P = 128
 NT = 512
+QUAD = 32
+D_WORDS = REST // QUAD // 2
 PASSES = BLK // 512
 MTILES = ROWS // P
 NTILES = REST // NT
 TILES = MTILES * NTILES
 LEAD_FIRST = 8
-WARM = 3
+WARM = 4
 S_BUFS = 3
 GROUP = 4
 F_CHUNKS = [(0, 2), (2, 5), (5, 8)]
@@ -58,7 +60,9 @@ def tile_lazy_pruning_update_k3_kernel(
         c_codes = [[kept("c_codes%d_%d" % (n, g), [P, NT], U32) for g in range(PASSES)] for n in range(NTILES)]
         c_plane = [[kept("c_plane%d_%d" % (n, g), [P, NT], U8) for g in range(PASSES)] for n in range(NTILES)]
         v_sb = [kept("v%d" % n, [P, MTILES, NT], BF16) for n in range(NTILES)]
-        d_col = kept("d_col", [P, REST // P], BF16)
+        d_part = kept("d_part", [P, REST // QUAD], BF16)
+        d_wide = kept("d_wide", [P, D_WORDS, QUAD], F32)
+        d_turned = kept("d_turned", [P, D_WORDS, QUAD], F32)
         d_row = kept("d_row", [P, NTILES, NT], BF16)
         ident = kept("ident", [P, P], F32)
         y_codes = [kept("y_codes%d" % n, [P, ROWS], U32) for n in range(NTILES)]
@@ -101,22 +105,22 @@ def tile_lazy_pruning_update_k3_kernel(
             nc.sync.dma_start(out=v_sb[n][:, lo:hi, :], in_=rows.rearrange("(m p) w -> p m w", p=P))
 
         load_b(nc.gpsimd, 0, 0, 1)
+        load_a(nc.gpsimd, 0)
         make_identity(nc, ident[:])
         for plane in (f_plane, b_first, a_first, ab_rest):
             nc.vector.memset(plane[:].rearrange("p g n -> p (g n)").bitcast(I32), 0)
-        nc.sync.dma_start(out=d_col[:], in_=d.rearrange("(p j) -> p j", p=P))
+        nc.sync.dma_start(out=d_part[:], in_=d.rearrange("(r j) -> r j", r=QUAD).partition_broadcast(P // QUAD))
         load_f_head(0)
         load_scales(nc.sync, f_plane, f_scales, 0)
         load_scales(nc.sync, b_first, b_scales[:, :, :NT], 4)
         load_f_head(1)
         load_b(nc.sync, 0, 1, 2)
-        load_a(nc.sync, 0)
         load_scales(nc.sync, a_first, a_scales[:, :, :NT], 0)
         load_f(1)
+        load_scales(nc.sync, ab_rest, b_scales[:, :, NT:], 4)
         load_c(0, 0)
         load_f(2)
         load_c(0, 1)
-        load_scales(nc.sync, ab_rest, b_scales[:, :, NT:], 4)
         load_scales(nc.sync, ab_rest, a_scales[:, :, NT:], 0)
         load_v(0, 0, 2)
         load_b(nc.sync, 1, 0, 2)
@@ -138,17 +142,16 @@ def tile_lazy_pruning_update_k3_kernel(
             bufs = {"ab": 3, "c": 3, "xt": 2}[kind]
             return psum.tile([P, NT], F32, name=kind, tag=kind, bufs=bufs)
 
-        d_words = d_col[:].bitcast(F32)
-        d_row_words = d_row[:].rearrange("r n w -> r (n w)").bitcast(F32).rearrange("r (p w) -> r p w", p=P)
-
-        def spread_d(w0, w1):
-            xt = bank("xt")
-            for w in range(w0, w1):
-                slot = w - w0
-                nc.tensor.transpose(
-                    xt[:, P * slot : P * (slot + 1)], d_words[:, w : w + 1].to_broadcast([P, P]), ident[:]
-                )
-            nc.scalar.copy(out=d_row_words[:, :, w0:w1], in_=xt[:, : P * (w1 - w0)].rearrange("r (w p) -> r p w", p=P))
+        def spread_d():
+            nc.scalar.copy(
+                out=d_wide[:].bitcast(U32),
+                in_=d_part[:].bitcast(U32).unsqueeze(2).to_broadcast([P, D_WORDS, QUAD]),
+            )
+            nc.vector.transpose(out=d_turned[:].rearrange("p j r -> p (j r)"), in_=d_wide[:].rearrange("p j w -> p (j w)"))
+            nc.scalar.copy(
+                out=d_row[:].rearrange("p n w -> p (n w)").bitcast(F32).rearrange("p (r j) -> p r j", r=QUAD),
+                in_=d_turned[:].rearrange("p j r -> p r j"),
+            )
 
         def f_operand(m, g):
             k = [lo <= m < hi for lo, hi in F_CHUNKS].index(True)
@@ -173,7 +176,7 @@ def tile_lazy_pruning_update_k3_kernel(
             n, m = divmod(i, MTILES)
             for g in passes:
                 if g == 0:
-                    ab_acc[i] = bank("ab")
+                    ab_acc[i] = bank("c" if 3 <= i < 6 else "ab")
                 mm(ab_acc[i], m, g, b_codes[n][:, g, :].bitcast(FP8X4), plane_of(b_first, n, g, 4), g == 0, False)
 
         def a_passes(i):
@@ -271,8 +274,7 @@ def tile_lazy_pruning_update_k3_kernel(
                         in_=y_plane[n][32 * q : 32 * q + 4, :].bitcast(I32),
                     )
 
-        spread_d(0, 4)
-        spread_d(4, 6)
+        spread_d()
         warm = bank("c")
         for k in range(WARM):
             lhs, lhs_scale = f_operand(0, 0)
@@ -295,11 +297,10 @@ def tile_lazy_pruning_update_k3_kernel(
             if i in (3, 5):
                 quantize_c(0, (3, 5).index(i))
         for i in range(S_BUFS):
-            subtract_from_v(nc.gpsimd, i)
+            subtract_from_v(nc.gpsimd if i else nc.vector, i)
 
         next_ab = LEAD_FIRST
-        last_group = TILES - GROUP
-        for j in range(last_group):
+        for j in range(20):
             n, m = divmod(j, MTILES)
             if n + 1 < NTILES and 1 <= m <= 4:
                 g, h = divmod(m - 1, 2)
@@ -307,18 +308,20 @@ def tile_lazy_pruning_update_k3_kernel(
             c_tile(j)
             turning = j > GROUP and j % GROUP == 1
             if n + 1 < NTILES and m in (4, 6):
-                quantize_c(n + 1, (m - 4) // 2)
+                quantize_c(n + 1, (4, 6).index(m))
             if j > GROUP and j % GROUP == 3:
                 quantize_y(j - 7, GROUP)
                 store_planes(j - 7, GROUP)
-            if turning:
+            if j in (5, 9, 13, 17):
                 subtract_from_v(nc.vector, j + S_BUFS)
+            if turning:
                 turn(j - 5, GROUP, "xt")
-            else:
+            if j not in (5, 9, 13, 17):
                 ab(next_ab)
                 next_ab += 1
+            if j not in (5, 9, 13, 17):
                 subtract_from_v(nc.gpsimd, j + S_BUFS)
-        subtract_from_v(nc.gpsimd, TILES - 1)
+        subtract_from_v(nc.gpsimd, 23)
         turn(16, 2, "xt")
         c_tile(20)
         c_tile(21)

@@ -1,7 +1,6 @@
 from contextlib import ExitStack
 
 import concourse.mybir as mybir
-from concourse.masks import make_identity
 
 ROWS, BLK, REST = 1024, 1024, 1536
 FLOPS = 3 * 2 * ROWS * BLK * REST
@@ -14,7 +13,9 @@ U8 = mybir.dt.uint8
 FP8X4 = mybir.dt.float8_e4m3fn_x4
 FP4X4 = mybir.dt.float4_e2m1fn_x4
 MULT = mybir.AluOpType.mult
+ADD = mybir.AluOpType.add
 SUB = mybir.AluOpType.subtract
+EQUAL = mybir.AluOpType.is_equal
 
 P = 128
 NT = 512
@@ -23,13 +24,24 @@ D_WORDS = REST // QUAD // 2
 PASSES = BLK // 512
 MTILES = ROWS // P
 NTILES = REST // NT
-TILES = MTILES * NTILES
-LEAD_FIRST = 8
-WARM = 4
-S_BUFS = 3
-GROUP = 4
+WIDE = REST - NT
 F_CHUNKS = [(0, 2), (2, 5), (5, 8)]
+V_FIRST = [(0, 2), (2, 4), (4, 6), (6, 8)]
+V_WIDE = [(0, 2), (2, 4), (4, 6), (6, 8)]
 HEAD_TILES = F_CHUNKS[0][1]
+LEAD = MTILES
+GROUP = 4
+WARM = 4
+B_ROW = 4
+PART_BUFS = 9
+Y_BUFS = 12
+BF_BUFS = 8
+GRP_BUFS = 5
+C_BUFS = 3
+S_BUFS = 3
+
+TILES = [(m, n) for n in range(NTILES) for m in range(MTILES)]
+AB_TILES = TILES
 
 
 def tile_lazy_pruning_update_k3_kernel(
@@ -48,21 +60,18 @@ def tile_lazy_pruning_update_k3_kernel(
         f_plane = kept("f_plane", [P, PASSES, ROWS], U8)
         a_first = kept("a_first", [P, PASSES, NT], U8)
         b_first = kept("b_first", [P, PASSES, NT], U8)
-        ab_rest = kept("ab_rest", [P, PASSES, REST - NT], U8)
+        ab_rest = kept("ab_rest", [P, PASSES, WIDE], U8)
         f_head = [kept("f_head%d" % g, [P, HEAD_TILES * P], U32) for g in range(PASSES)]
         f_codes = [kept("f_codes%d" % lo, [P, PASSES, (hi - lo) * P], U32) if lo else None for lo, hi in F_CHUNKS]
         a_codes = [kept("a_codes%d" % n, [P, PASSES, 2 * NT], U8) for n in range(NTILES)]
-        b_codes = [kept("b_codes%d" % n, [P, PASSES, NT], U32) for n in range(NTILES)]
+        b_head = [kept("b_head%d" % g, [P, NT], U32) for g in range(PASSES)]
+        b_codes = [kept("b_codes%d" % n, [P, PASSES, NT], U32) if n else None for n in range(NTILES)]
         c_raw = [[kept("c_raw%d_%d" % (n, g), [P, 4, NT], BF16) for g in range(PASSES)] for n in range(NTILES)]
-        c_grp = [[kept("c_grp%d_%d" % (n, g), [P, NT, 4], BF16) if (n, g) != (0, 1) else None for g in range(PASSES)]
-                 for n in range(NTILES)]
-        c_grp[0][1] = work.tile([P, NT, 4], BF16, name="c_grp0_1", tag="shared", bufs=1, align_bytes=64)
         c_codes = [[kept("c_codes%d_%d" % (n, g), [P, NT], U32) for g in range(PASSES)] for n in range(NTILES)]
         c_plane = [[kept("c_plane%d_%d" % (n, g), [P, NT], U8) for g in range(PASSES)] for n in range(NTILES)]
-        v_sb = [kept("v%d" % n, [P, MTILES, NT], BF16) for n in range(NTILES)]
+        v_first = [kept("v_first%d" % lo, [P, hi - lo, NT], BF16) for lo, hi in V_FIRST]
+        v_wide = [kept("v_wide%d" % lo, [P, hi - lo, WIDE], BF16) for lo, hi in V_WIDE]
         d_part = kept("d_part", [P, REST // QUAD], BF16)
-        d_wide = kept("d_wide", [P, D_WORDS, QUAD], F32)
-        d_turned = kept("d_turned", [P, D_WORDS, QUAD], F32)
         d_row = kept("d_row", [P, NTILES, NT], BF16)
         ident = kept("ident", [P, P], F32)
         y_codes = [kept("y_codes%d" % n, [P, ROWS], U32) for n in range(NTILES)]
@@ -72,77 +81,74 @@ def tile_lazy_pruning_update_k3_kernel(
         a_view = a_words.rearrange("g p x -> p g x")
         b_view = b_words.rearrange("g p n t -> p g (n t)")
 
+        def move(queue, dst, src):
+            queue.dma_start(out=dst.bitcast(I32), in_=src.bitcast(I32))
+
         def load_scales(queue, plane, scales, first_row):
             for q in range(4):
-                lo = 32 * q + first_row
-                queue.dma_start(
-                    out=plane[lo : lo + 4, :, :].bitcast(I32),
-                    in_=scales[:, 4 * q : 4 * q + 4, :].rearrange("g r n -> r g n").bitcast(I32),
-                )
+                lo = QUAD * q + first_row
+                move(queue, plane[lo : lo + 4, :, :], scales[:, 4 * q : 4 * q + 4, :].rearrange("g r n -> r g n"))
 
         def load_f(k):
             lo, hi = F_CHUNKS[k]
-            nc.sync.dma_start(out=f_codes[k][:].bitcast(I32), in_=f_view[:, :, 4 * P * lo : 4 * P * hi].bitcast(I32))
-
-        def load_f_head(g):
-            nc.sync.dma_start(out=f_head[g][:].bitcast(I32), in_=f_view[:, g, : 4 * P * HEAD_TILES].bitcast(I32))
+            move(nc.sync, f_codes[k][:], f_view[:, :, 4 * P * lo : 4 * P * hi])
 
         def load_a(queue, n):
-            queue.dma_start(out=a_codes[n][:].bitcast(I32), in_=a_view[:, :, 2 * NT * n : 2 * NT * (n + 1)].bitcast(I32))
+            move(queue, a_codes[n][:], a_view[:, :, 2 * NT * n : 2 * NT * (n + 1)])
 
-        def load_b(queue, n, g0, g1):
-            queue.dma_start(
-                out=b_codes[n][:, g0:g1, :].bitcast(I32),
-                in_=b_view[:, g0:g1, 4 * NT * n : 4 * NT * (n + 1)].bitcast(I32),
-            )
+        def load_b(n):
+            move(nc.sync, b_codes[n][:], b_view[:, :, 4 * NT * n : 4 * NT * (n + 1)])
 
         def load_c(n, g):
             rows = c[512 * g : 512 * (g + 1), NT * n : NT * (n + 1)]
             nc.sync.dma_start(out=c_raw[n][g][:], in_=rows.rearrange("(p j) w -> p j w", j=4))
 
-        def load_v(n, lo, hi):
-            rows = v[P * lo : P * hi, NT * n : NT * (n + 1)]
-            nc.sync.dma_start(out=v_sb[n][:, lo:hi, :], in_=rows.rearrange("(m p) w -> p m w", p=P))
+        def load_v(tile, tiles, cols):
+            nc.sync.dma_start(out=tile[:], in_=v[P * tiles[0] : P * tiles[1], cols].rearrange("(m p) w -> p m w", p=P))
 
-        load_b(nc.gpsimd, 0, 0, 1)
+        first_cols, wide_cols = slice(0, NT), slice(NT, REST)
+
+        move(nc.gpsimd, b_head[0][:], b_view[:, 0, : 4 * NT])
         load_a(nc.gpsimd, 0)
-        make_identity(nc, ident[:])
         for plane in (f_plane, b_first, a_first, ab_rest):
             nc.vector.memset(plane[:].rearrange("p g n -> p (g n)").bitcast(I32), 0)
+        load_scales(nc.gpsimd, ab_rest, b_scales[:, :, wide_cols], B_ROW)
         nc.sync.dma_start(out=d_part[:], in_=d.rearrange("(r j) -> r j", r=QUAD).partition_broadcast(P // QUAD))
-        load_f_head(0)
+        move(nc.sync, f_head[0][:], f_view[:, 0, : 4 * P * HEAD_TILES])
         load_scales(nc.sync, f_plane, f_scales, 0)
-        load_scales(nc.sync, b_first, b_scales[:, :, :NT], 4)
-        load_f_head(1)
-        load_b(nc.sync, 0, 1, 2)
-        load_scales(nc.sync, a_first, a_scales[:, :, :NT], 0)
+        load_scales(nc.sync, b_first, b_scales[:, :, first_cols], B_ROW)
+        move(nc.sync, f_head[1][:], f_view[:, 1, : 4 * P * HEAD_TILES])
+        move(nc.sync, b_head[1][:], b_view[:, 1, : 4 * NT])
+        load_scales(nc.sync, a_first, a_scales[:, :, first_cols], 0)
         load_f(1)
-        load_scales(nc.sync, ab_rest, b_scales[:, :, NT:], 4)
         load_c(0, 0)
         load_f(2)
         load_c(0, 1)
-        load_scales(nc.sync, ab_rest, a_scales[:, :, NT:], 0)
-        load_v(0, 0, 2)
-        load_b(nc.sync, 1, 0, 2)
+        load_scales(nc.sync, ab_rest, a_scales[:, :, wide_cols], 0)
+        load_v(v_first[0], V_FIRST[0], first_cols)
+        load_b(1)
         load_a(nc.sync, 1)
-        load_v(0, 2, 4)
+        load_v(v_first[1], V_FIRST[1], first_cols)
         load_c(1, 0)
-        load_v(0, 4, 8)
+        load_v(v_first[2], V_FIRST[2], first_cols)
+        load_v(v_first[3], V_FIRST[3], first_cols)
         load_c(1, 1)
-        load_v(1, 0, 4)
-        load_b(nc.sync, 2, 0, 2)
+        load_v(v_wide[0], V_WIDE[0], wide_cols)
+        load_v(v_wide[1], V_WIDE[1], wide_cols)
+        load_b(2)
         load_a(nc.sync, 2)
         load_c(2, 0)
+        load_v(v_wide[2], V_WIDE[2], wide_cols)
         load_c(2, 1)
-        load_v(1, 4, 8)
-        load_v(2, 0, 4)
-        load_v(2, 4, 8)
+        load_v(v_wide[3], V_WIDE[3], wide_cols)
 
         def bank(kind):
             bufs = {"ab": 3, "c": 3, "xt": 2}[kind]
             return psum.tile([P, NT], F32, name=kind, tag=kind, bufs=bufs)
 
         def spread_d():
+            d_wide = work.tile([P, D_WORDS, QUAD], F32, name="d_wide", tag="c_grp", bufs=C_BUFS, align_bytes=64)
+            d_turned = work.tile([P, D_WORDS, QUAD], F32, name="d_turned", tag="c_grp", bufs=C_BUFS, align_bytes=64)
             nc.scalar.copy(
                 out=d_wide[:].bitcast(U32),
                 in_=d_part[:].bitcast(U32).unsqueeze(2).to_broadcast([P, D_WORDS, QUAD]),
@@ -153,10 +159,26 @@ def tile_lazy_pruning_update_k3_kernel(
                 in_=d_turned[:].rearrange("p j r -> p r j"),
             )
 
+        def build_identity():
+            ones = kept("ones", [P, QUAD], F32)
+            ramp = kept("ramp", [P, QUAD], F32)
+            ramp_turned = kept("ramp_turned", [P, QUAD], F32)
+            nc.vector.memset(ones[:], 1.0)
+            nc.vector.memset(ident[:], 0.0)
+            nc.vector.tensor_tensor_scan(out=ramp[:], data0=ones[:], data1=ones[:], initial=0.0, op0=MULT, op1=ADD)
+            nc.vector.transpose(out=ramp_turned[:], in_=ramp[:])
+            for q in range(P // QUAD):
+                rows = slice(QUAD * q, QUAD * (q + 1))
+                nc.vector.tensor_tensor(out=ident[rows, rows], in0=ramp[rows, :], in1=ramp_turned[rows, :], op=EQUAL)
+
+        def chunk_of(chunks, m):
+            k = [lo <= m < hi for lo, hi in chunks].index(True)
+            return k, m - chunks[k][0]
+
         def f_operand(m, g):
-            k = [lo <= m < hi for lo, hi in F_CHUNKS].index(True)
-            off = (m - F_CHUNKS[k][0]) * P
-            codes = f_codes[k][:, g, off : off + P] if k else f_head[g][:, off : off + P]
+            k, off = chunk_of(F_CHUNKS, m)
+            cols = slice(P * off, P * (off + 1))
+            codes = f_codes[k][:, g, cols] if k else f_head[g][:, cols]
             return codes.bitcast(FP8X4), f_plane[:, g, P * m : P * (m + 1)]
 
         def mm(acc, m, g, rhs, rhs_scale, start, stop):
@@ -165,74 +187,116 @@ def tile_lazy_pruning_update_k3_kernel(
                 out=acc[:], lhsT=lhs, lhsT_scale=lhs_scale, rhs=rhs, rhs_scale=rhs_scale, start=start, stop=stop
             )
 
-        ab_acc, t_sb, s_sb, y_bf, y_grp = {}, {}, {}, {}, {}
+        ab_acc, part, y_bf, y_grp, c_grp, y_done = {}, {}, {}, {}, {}, {}
 
         def plane_of(first, n, g, row):
-            if n == 0:
-                return first[row:P, g, :]
-            return ab_rest[row:P, g, NT * (n - 1) : NT * n]
+            return first[row:P, g, :] if n == 0 else ab_rest[row:P, g, NT * (n - 1) : NT * n]
 
-        def b_passes(i, passes=range(PASSES)):
-            n, m = divmod(i, MTILES)
-            for g in passes:
-                if g == 0:
-                    ab_acc[i] = bank("c" if 3 <= i < 6 else "ab")
-                mm(ab_acc[i], m, g, b_codes[n][:, g, :].bitcast(FP8X4), plane_of(b_first, n, g, 4), g == 0, False)
+        def b_pass(i, g):
+            m, n = AB_TILES[i]
+            if g == 0:
+                ab_acc[i] = bank("c" if 3 <= i < 6 else "ab")
+            codes = b_codes[n][:, g, :] if n else b_head[g][:]
+            mm(ab_acc[i], m, g, codes.bitcast(FP8X4), plane_of(b_first, n, g, B_ROW), g == 0, False)
 
         def a_passes(i):
-            n, m = divmod(i, MTILES)
+            m, n = AB_TILES[i]
             for g in range(PASSES):
                 mm(ab_acc[i], m, g, a_codes[n][:, g, :].bitcast(FP4X4), plane_of(a_first, n, g, 0), False, g == PASSES - 1)
 
         def scale_ab(i):
-            n = i // MTILES
-            t_sb[i] = work.tile([P, NT], F32, name="t", tag="t", bufs=9)
-            nc.vector.tensor_tensor(out=t_sb[i][:], in0=d_row[:, n, :], in1=ab_acc[i][:], op=MULT)
-
-        def subtract_from_v(engine, i):
-            n, m = divmod(i, MTILES)
-            tag, bufs = {0: ("shared", 1), TILES - 1: ("s_last", 1)}.get(i, ("s", S_BUFS))
-            s_sb[i] = work.tile([P, NT], F32, name=tag, tag=tag, bufs=bufs, align_bytes=64)
-            engine.tensor_tensor(out=s_sb[i][:], in0=v_sb[n][:, m, :], in1=t_sb[i][:], op=SUB)
+            tile = AB_TILES[i]
+            part[tile] = work.tile([P, NT], F32, name="part", tag="part", bufs=PART_BUFS)
+            nc.vector.tensor_tensor(out=part[tile][:], in0=d_row[:, tile[1], :], in1=ab_acc[i][:], op=MULT)
 
         def ab(i):
-            b_passes(i)
+            for g in range(PASSES):
+                b_pass(i, g)
             a_passes(i)
             scale_ab(i)
+
+        def v_of(tile):
+            m, n = tile
+            if n == 0:
+                k, off = chunk_of(V_FIRST, m)
+                return v_first[k][:, off, :]
+            k, off = chunk_of(V_WIDE, m)
+            return v_wide[k][:, off, NT * (n - 1) : NT * n]
+
+        def y_of(tile):
+            return work.tile([P, NT], F32, name="y", tag="y", bufs=Y_BUFS)[:]
+
+        def store_y(tile, y):
+            m, n = tile
+            nc.sync.dma_start(out=out_0[P * m : P * (m + 1), NT * n : NT * (n + 1)], in_=y)
 
         def word_order(ap):
             return ap.rearrange("r (p u e) -> r u p e", u=2, e=2)
 
-        def c_tile(j):
-            n, m = divmod(j, MTILES)
+        def c_passes(j):
+            m, n = TILES[j]
             acc = bank("c")
             for g in range(PASSES):
                 mm(acc, m, g, c_codes[n][g][:].bitcast(FP8X4), c_plane[n][g][:], g == 0, g == PASSES - 1)
-            y = work.tile([P, NT], F32, name="y", tag="y", bufs=12)
-            y_bf[j] = work.tile([P, 2, P, 2], BF16, name="y_bf", tag="y_bf", bufs=8, align_bytes=64)
-            if j == TILES - 1:
-                nc.vector.tensor_tensor(out=y_bf[j][:], in0=word_order(s_sb[j][:]), in1=word_order(acc[:]), op=SUB)
-            nc.vector.tensor_tensor(out=y[:], in0=s_sb[j][:], in1=acc[:], op=SUB)
-            nc.sync.dma_start(out=out_0[P * m : P * (m + 1), NT * n : NT * (n + 1)], in_=y[:])
-            if j < TILES - 1:
-                nc.scalar.copy(out=y_bf[j][:], in_=word_order(y[:]))
+            return acc
+
+        def rounded(j):
+            y_bf[j] = work.tile([P, 2, P, 2], BF16, name="y_bf", tag="y_bf", bufs=BF_BUFS, align_bytes=64)
+            return y_bf[j][:]
+
+        def add_c(j):
+            tile = TILES[j]
+            acc = c_passes(j)
+            nc.vector.tensor_tensor(out=part[tile][:], in0=part[tile][:], in1=acc[:], op=ADD)
+
+        def finish(engine, j):
+            tile = TILES[j]
+            y = y_of(tile)
+            engine.tensor_tensor(out=y, in0=v_of(tile), in1=part[tile][:], op=SUB)
+            store_y(tile, y)
+            y_done[j] = y
+
+        def round_y(j):
+            nc.scalar.copy(out=rounded(j), in_=word_order(y_done[j]))
+
+        def subtract_early(engine, j):
+            tile = TILES[j]
+            tag, bufs = {1: ("shared", 1), len(TILES) - 1: ("s_last", 1)}.get(j, ("s", S_BUFS))
+            s = work.tile([P, NT], F32, name=tag, tag=tag, bufs=bufs, align_bytes=64)
+            engine.tensor_tensor(out=s[:], in0=v_of(tile), in1=part[tile][:], op=SUB)
+            part[tile] = s
+
+        def finish_late(j):
+            tile = TILES[j]
+            acc = c_passes(j)
+            y = y_of(tile)
+            last = j == len(TILES) - 1
+            if last:
+                nc.vector.tensor_tensor(out=rounded(j), in0=word_order(part[tile][:]), in1=word_order(acc[:]), op=SUB)
+            nc.vector.tensor_tensor(out=y, in0=part[tile][:], in1=acc[:], op=SUB)
+            store_y(tile, y)
+            y_done[j] = y
 
         def interleave(engine_copy, n, g, h):
+            if (n, g) not in c_grp:
+                tag, bufs = ("shared", 1) if (n, g) == (0, PASSES - 1) else ("c_grp", C_BUFS)
+                c_grp[n, g] = work.tile([P, NT, 4], BF16, name="c_grp", tag=tag, bufs=bufs, align_bytes=64)
+            raw = c_raw[n][g]
             cols = slice(h * NT // 2, (h + 1) * NT // 2)
             engine_copy(
-                out=c_grp[n][g][:, cols, :].rearrange("p (c i) t -> p c t i", i=4),
-                in_=c_raw[n][g][:, :, cols].rearrange("p t (c i) -> p c t i", i=4),
+                out=c_grp[n, g][:, cols, :].rearrange("p (c i) t -> p c t i", i=4),
+                in_=raw[:, :, cols].rearrange("p t (c i) -> p c t i", i=4),
             )
 
         def quantize_c(n, g):
             nc.vector.quantize_mx(
                 out=c_codes[n][g][:].bitcast(FP8X4),
                 scales=c_plane[n][g][:],
-                in_=c_grp[n][g][:].rearrange("p w t -> p (w t)"),
+                in_=c_grp[n, g][:].rearrange("p w t -> p (w t)"),
             )
 
         def turn(first, count, kind):
-            grp = work.tile([P, count * P, 4], BF16, name="y_grp", tag="y_grp", bufs=5, align_bytes=64)
+            grp = work.tile([P, count * P, 4], BF16, name="y_grp", tag="y_grp", bufs=GRP_BUFS, align_bytes=64)
             y_grp[first] = grp
             grp_words = grp[:].rearrange("p m t -> p (m t)").bitcast(F32)
             banks = []
@@ -251,91 +315,171 @@ def tile_lazy_pruning_update_k3_kernel(
                     in_=xt[:, : 2 * P * span].rearrange("p (s u r) -> p s r u", r=P, u=2),
                 )
 
-        def quantize_y(first, count):
-            n, m = divmod(first, MTILES)
+        def quantize_y(first, lo, count):
+            m, n = TILES[first + lo]
             cols = slice(P * m, P * (m + count))
             nc.vector.quantize_mx(
                 out=y_codes[n][:, cols].bitcast(FP8X4),
                 scales=y_plane[n][:, cols],
-                in_=y_grp[first][:].rearrange("p m t -> p (m t)"),
+                in_=y_grp[first][:, P * lo : P * (lo + count), :].rearrange("p m t -> p (m t)"),
             )
 
-        def store_planes(first, count):
-            n, m = divmod(first, MTILES)
-            cols = slice(P * m, P * (m + count))
-            nc.sync.dma_start(
-                out=out_1[n].rearrange("p m t -> p (m t)")[:, 4 * P * m : 4 * P * (m + count)].bitcast(I32),
-                in_=y_codes[n][:, cols].bitcast(I32),
-            )
-            if m + count == MTILES:
-                for q in range(4):
-                    nc.sync.dma_start(
-                        out=out_2[n, 4 * q : 4 * q + 4, :].bitcast(I32),
-                        in_=y_plane[n][32 * q : 32 * q + 4, :].bitcast(I32),
-                    )
+        def store_codes(n, lo, hi):
+            move(nc.sync, out_1[n].rearrange("p m t -> p (m t)")[:, 4 * P * lo : 4 * P * hi], y_codes[n][:, P * lo : P * hi])
 
+        def store_scales(n):
+            for q in range(4):
+                move(nc.sync, out_2[n, 4 * q : 4 * q + 4, :], y_plane[n][QUAD * q : QUAD * q + 4, :])
+
+        build_identity()
         spread_d()
         warm = bank("c")
         for k in range(WARM):
             lhs, lhs_scale = f_operand(0, 0)
             nc.tensor.matmul_mx(
-                out=warm[:, : 2 * P], lhsT=lhs, lhsT_scale=lhs_scale, rhs=f_head[0][:, : 2 * P].bitcast(FP8X4),
+                out=warm[:, : 2 * P], lhsT=lhs, lhsT_scale=lhs_scale, rhs=f_head[0][:].bitcast(FP8X4),
                 rhs_scale=f_plane[:, 0, : 2 * P], start=True, stop=True,
             )
         for g in range(PASSES):
             for i in range(HEAD_TILES):
-                b_passes(i, [g])
+                b_pass(i, g)
         for g in range(PASSES):
             interleave(nc.scalar.copy, 0, g, 1)
         for i in range(HEAD_TILES):
             a_passes(i)
             scale_ab(i)
-        for i in range(HEAD_TILES, LEAD_FIRST):
+        for i in range(HEAD_TILES, LEAD):
             ab(i)
-            if i in (2, 4):
-                interleave(nc.vector.tensor_copy, 0, (2, 4).index(i), 0)
-            if i in (3, 5):
-                quantize_c(0, (3, 5).index(i))
-        for i in range(S_BUFS):
-            subtract_from_v(nc.gpsimd if i else nc.vector, i)
+            g, step = divmod(i - HEAD_TILES, 2)
+            if g < PASSES:
+                if step == 0:
+                    interleave(nc.vector.tensor_copy, 0, g, 0)
+                else:
+                    quantize_c(0, g)
 
-        next_ab = LEAD_FIRST
-        for j in range(20):
-            n, m = divmod(j, MTILES)
-            if n + 1 < NTILES and 1 <= m <= 4:
-                g, h = divmod(m - 1, 2)
-                interleave(nc.scalar.copy, n + 1, g, h)
-            c_tile(j)
-            turning = j > GROUP and j % GROUP == 1
-            if n + 1 < NTILES and m in (4, 6):
-                quantize_c(n + 1, (4, 6).index(m))
-            if j > GROUP and j % GROUP == 3:
-                quantize_y(j - 7, GROUP)
-                store_planes(j - 7, GROUP)
-            if j in (5, 9, 13, 17):
-                subtract_from_v(nc.vector, j + S_BUFS)
-            if turning:
-                turn(j - 5, GROUP, "xt")
-            if j not in (5, 9, 13, 17):
-                ab(next_ab)
-                next_ab += 1
-            if j not in (5, 9, 13, 17):
-                subtract_from_v(nc.gpsimd, j + S_BUFS)
-        subtract_from_v(nc.gpsimd, 23)
+        subtract_early(nc.vector, 0)
+        subtract_early(nc.gpsimd, 1)
+        subtract_early(nc.gpsimd, 2)
+        finish_late(0)
+        round_y(0)
+        ab(8)
+        subtract_early(nc.gpsimd, 3)
+        interleave(nc.scalar.copy, 1, 0, 0)
+        finish_late(1)
+        round_y(1)
+        ab(9)
+        subtract_early(nc.gpsimd, 4)
+        interleave(nc.scalar.copy, 1, 0, 1)
+        finish_late(2)
+        round_y(2)
+        ab(10)
+        subtract_early(nc.gpsimd, 5)
+        interleave(nc.scalar.copy, 1, 1, 0)
+        finish_late(3)
+        round_y(3)
+        ab(11)
+        subtract_early(nc.gpsimd, 6)
+        interleave(nc.scalar.copy, 1, 1, 1)
+        finish_late(4)
+        round_y(4)
+        quantize_c(1, 0)
+        ab(12)
+        subtract_early(nc.gpsimd, 7)
+        finish_late(5)
+        round_y(5)
+        subtract_early(nc.vector, 8)
+        turn(0, 4, "xt")
+        finish_late(6)
+        round_y(6)
+        quantize_c(1, 1)
+        ab(13)
+        subtract_early(nc.gpsimd, 9)
+        finish_late(7)
+        round_y(7)
+        quantize_y(0, 0, 4)
+        ab(14)
+        subtract_early(nc.gpsimd, 10)
+        finish_late(8)
+        round_y(8)
+        ab(15)
+        subtract_early(nc.gpsimd, 11)
+        interleave(nc.scalar.copy, 2, 0, 0)
+        finish_late(9)
+        round_y(9)
+        subtract_early(nc.vector, 12)
+        turn(4, 4, "xt")
+        interleave(nc.scalar.copy, 2, 0, 1)
+        finish_late(10)
+        round_y(10)
+        ab(16)
+        subtract_early(nc.gpsimd, 13)
+        interleave(nc.scalar.copy, 2, 1, 0)
+        finish_late(11)
+        round_y(11)
+        quantize_y(4, 0, 4)
+        store_codes(0, 0, 8)
+        store_scales(0)
+        ab(17)
+        subtract_early(nc.gpsimd, 14)
+        interleave(nc.scalar.copy, 2, 1, 1)
+        finish_late(12)
+        round_y(12)
+        quantize_c(2, 0)
+        ab(18)
+        subtract_early(nc.gpsimd, 15)
+        finish_late(13)
+        round_y(13)
+        subtract_early(nc.vector, 16)
+        turn(8, 4, "xt")
+        finish_late(14)
+        round_y(14)
+        quantize_c(2, 1)
+        ab(19)
+        subtract_early(nc.gpsimd, 17)
+        finish_late(15)
+        round_y(15)
+        quantize_y(8, 0, 4)
+        store_codes(1, 0, 4)
+        ab(20)
+        subtract_early(nc.gpsimd, 18)
+        finish_late(16)
+        round_y(16)
+        ab(21)
+        subtract_early(nc.gpsimd, 19)
+        finish_late(17)
+        round_y(17)
+        subtract_early(nc.vector, 20)
+        turn(12, 4, "xt")
+        finish_late(18)
+        round_y(18)
+        ab(22)
+        subtract_early(nc.gpsimd, 21)
+        finish_late(19)
+        round_y(19)
+        quantize_y(12, 0, 4)
+        store_codes(1, 4, 8)
+        store_scales(1)
+        ab(23)
+        subtract_early(nc.gpsimd, 22)
+        subtract_early(nc.gpsimd, 23)
         turn(16, 2, "xt")
-        c_tile(20)
-        c_tile(21)
+        finish_late(20)
+        round_y(20)
+        finish_late(21)
+        round_y(21)
         turn(18, 2, "xt")
-        quantize_y(16, 2)
-        c_tile(22)
-        c_tile(23)
+        quantize_y(16, 0, 2)
+        finish_late(22)
+        round_y(22)
+        finish_late(23)
         turn(20, 2, "ab")
         turn(22, 1, "ab")
         turn(23, 1, "ab")
-        quantize_y(18, 2)
-        store_planes(16, 4)
-        quantize_y(20, 2)
-        quantize_y(22, 1)
-        store_planes(20, 3)
-        quantize_y(23, 1)
-        store_planes(23, 1)
+        quantize_y(18, 0, 2)
+        store_codes(2, 0, 4)
+        quantize_y(20, 0, 2)
+        quantize_y(22, 0, 1)
+        store_codes(2, 4, 7)
+        quantize_y(23, 0, 1)
+        store_codes(2, 7, 8)
+        store_scales(2)

@@ -20,7 +20,7 @@ EQUAL = mybir.AluOpType.is_equal
 P = 128
 NT = 512
 QUAD = 32
-D_WORDS = REST // QUAD // 2
+D_WORDS = REST // P // 2
 PASSES = BLK // 512
 MTILES = ROWS // P
 NTILES = REST // NT
@@ -71,7 +71,7 @@ def tile_lazy_pruning_update_k3_kernel(
         c_plane = [[kept("c_plane%d_%d" % (n, g), [P, NT], U8) for g in range(PASSES)] for n in range(NTILES)]
         v_first = [kept("v_first%d" % lo, [P, hi - lo, NT], BF16) for lo, hi in V_FIRST]
         v_wide = [kept("v_wide%d" % lo, [P, hi - lo, WIDE], BF16) for lo, hi in V_WIDE]
-        d_part = kept("d_part", [P, REST // QUAD], BF16)
+        d_col = kept("d_col", [P, REST // P], BF16)
         d_row = kept("d_row", [P, NTILES, NT], BF16)
         ident = kept("ident", [P, P], F32)
         y_codes = [kept("y_codes%d" % n, [P, ROWS], U32) for n in range(NTILES)]
@@ -106,14 +106,32 @@ def tile_lazy_pruning_update_k3_kernel(
         def load_v(tile, tiles, cols):
             nc.sync.dma_start(out=tile[:], in_=v[P * tiles[0] : P * tiles[1], cols].rearrange("(m p) w -> p m w", p=P))
 
+        def build_identity():
+            ones = kept("ones", [P, QUAD], F32)
+            ramp = kept("ramp", [P, QUAD], F32)
+            ramp_turned = kept("ramp_turned", [P, QUAD], F32)
+            nc.vector.memset(ones[:], 1.0)
+            nc.vector.memset(ident[:], 0.0)
+            nc.vector.tensor_tensor_scan(out=ramp[:], data0=ones[:], data1=ones[:], initial=0.0, op0=MULT, op1=ADD)
+            nc.vector.transpose(out=ramp_turned[:], in_=ramp[:])
+            for q in range(P // QUAD):
+                rows = slice(QUAD * q, QUAD * (q + 1))
+                nc.vector.tensor_tensor(out=ident[rows, rows], in0=ramp[rows, :], in1=ramp_turned[rows, :], op=EQUAL)
+
+        def zero(plane):
+            nc.vector.memset(plane[:].rearrange("p g n -> p (g n)").bitcast(I32), 0)
+
         first_cols, wide_cols = slice(0, NT), slice(NT, REST)
 
         move(nc.gpsimd, b_head[0][:], b_view[:, 0, : 4 * NT])
         load_a(nc.gpsimd, 0)
-        for plane in (f_plane, b_first, a_first, ab_rest):
-            nc.vector.memset(plane[:].rearrange("p g n -> p (g n)").bitcast(I32), 0)
+        zero(f_plane)
+        zero(b_first)
+        build_identity()
+        zero(a_first)
+        zero(ab_rest)
         load_scales(nc.gpsimd, ab_rest, b_scales[:, :, wide_cols], B_ROW)
-        nc.sync.dma_start(out=d_part[:], in_=d.rearrange("(r j) -> r j", r=QUAD).partition_broadcast(P // QUAD))
+        nc.sync.dma_start(out=d_col[:], in_=d.rearrange("(p j) -> p j", p=P))
         move(nc.sync, f_head[0][:], f_view[:, 0, : 4 * P * HEAD_TILES])
         load_scales(nc.sync, f_plane, f_scales, 0)
         load_scales(nc.sync, b_first, b_scales[:, :, first_cols], B_ROW)
@@ -147,29 +165,14 @@ def tile_lazy_pruning_update_k3_kernel(
             return psum.tile([P, NT], F32, name=kind, tag=kind, bufs=bufs)
 
         def spread_d():
-            d_wide = work.tile([P, D_WORDS, QUAD], F32, name="d_wide", tag="c_grp", bufs=C_BUFS, align_bytes=64)
-            d_turned = work.tile([P, D_WORDS, QUAD], F32, name="d_turned", tag="c_grp", bufs=C_BUFS, align_bytes=64)
-            nc.scalar.copy(
-                out=d_wide[:].bitcast(U32),
-                in_=d_part[:].bitcast(U32).unsqueeze(2).to_broadcast([P, D_WORDS, QUAD]),
-            )
-            nc.vector.transpose(out=d_turned[:].rearrange("p j r -> p (j r)"), in_=d_wide[:].rearrange("p j w -> p (j w)"))
-            nc.scalar.copy(
-                out=d_row[:].rearrange("p n w -> p (n w)").bitcast(F32).rearrange("p (r j) -> p r j", r=QUAD),
-                in_=d_turned[:].rearrange("p j r -> p r j"),
-            )
-
-        def build_identity():
-            ones = kept("ones", [P, QUAD], F32)
-            ramp = kept("ramp", [P, QUAD], F32)
-            ramp_turned = kept("ramp_turned", [P, QUAD], F32)
-            nc.vector.memset(ones[:], 1.0)
-            nc.vector.memset(ident[:], 0.0)
-            nc.vector.tensor_tensor_scan(out=ramp[:], data0=ones[:], data1=ones[:], initial=0.0, op0=MULT, op1=ADD)
-            nc.vector.transpose(out=ramp_turned[:], in_=ramp[:])
-            for q in range(P // QUAD):
-                rows = slice(QUAD * q, QUAD * (q + 1))
-                nc.vector.tensor_tensor(out=ident[rows, rows], in0=ramp[rows, :], in1=ramp_turned[rows, :], op=EQUAL)
+            d_words = d_col[:].bitcast(F32)
+            d_row_words = d_row[:].rearrange("r n w -> r (n w)").bitcast(F32).rearrange("r (p w) -> r p w", p=P)
+            for lo, hi in ((0, 4), (4, D_WORDS)):
+                xt = bank("xt")
+                for w in range(lo, hi):
+                    slot = slice(P * (w - lo), P * (w - lo + 1))
+                    nc.tensor.transpose(xt[:, slot], d_words[:, w : w + 1].to_broadcast([P, P]), ident[:])
+                nc.scalar.copy(out=d_row_words[:, :, lo:hi], in_=xt[:, : P * (hi - lo)].rearrange("r (w p) -> r p w", p=P))
 
         def chunk_of(chunks, m):
             k = [lo <= m < hi for lo, hi in chunks].index(True)
@@ -329,9 +332,8 @@ def tile_lazy_pruning_update_k3_kernel(
 
         def store_scales(n):
             for q in range(4):
-                move(nc.sync, out_2[n, 4 * q : 4 * q + 4, :], y_plane[n][QUAD * q : QUAD * q + 4, :])
+                move(nc.scalar if n == NTILES - 1 and q % 2 else nc.sync, out_2[n, 4 * q : 4 * q + 4, :], y_plane[n][QUAD * q : QUAD * q + 4, :])
 
-        build_identity()
         spread_d()
         warm = bank("c")
         for k in range(WARM):
@@ -478,8 +480,8 @@ def tile_lazy_pruning_update_k3_kernel(
         quantize_y(18, 0, 2)
         store_codes(2, 0, 4)
         quantize_y(20, 0, 2)
+        store_codes(2, 4, 6)
         quantize_y(22, 0, 1)
-        store_codes(2, 4, 7)
         quantize_y(23, 0, 1)
-        store_codes(2, 7, 8)
+        store_codes(2, 6, 8)
         store_scales(2)

@@ -36,9 +36,9 @@ B_ROW = 4
 PART_BUFS = 9
 Y_BUFS = 12
 BF_BUFS = 8
-GRP_BUFS = 5
+GRP_BUFS = 6
 C_BUFS = 3
-S_BUFS = 3
+S_AHEAD = 3
 
 TILES = [(m, n) for n in range(NTILES) for m in range(MTILES)]
 AB_TILES = TILES
@@ -190,6 +190,7 @@ def tile_lazy_pruning_update_k3_kernel(
                 out=acc[:], lhsT=lhs, lhsT_scale=lhs_scale, rhs=rhs, rhs_scale=rhs_scale, start=start, stop=stop
             )
 
+        s_slot = {}
         ab_acc, part, y_bf, y_grp, c_grp, y_done = {}, {}, {}, {}, {}, {}
 
         def plane_of(first, n, g, row):
@@ -262,10 +263,10 @@ def tile_lazy_pruning_update_k3_kernel(
         def round_y(j):
             nc.scalar.copy(out=rounded(j), in_=word_order(y_done[j]))
 
-        def subtract_early(engine, j):
+        def subtract_early(engine, j, slot=None):
             tile = TILES[j]
-            tag, bufs = {1: ("shared", 1), len(TILES) - 1: ("s_last", 1)}.get(j, ("s", S_BUFS))
-            s = work.tile([P, NT], F32, name=tag, tag=tag, bufs=bufs, align_bytes=64)
+            tag = s_slot[j] = slot or s_slot[j - S_AHEAD]
+            s = work.tile([P, NT], F32, name=tag, tag=tag, bufs=1, align_bytes=64)
             engine.tensor_tensor(out=s[:], in0=v_of(tile), in1=part[tile][:], op=SUB)
             part[tile] = s
 
@@ -345,23 +346,25 @@ def tile_lazy_pruning_update_k3_kernel(
         for g in range(PASSES):
             for i in range(HEAD_TILES):
                 b_pass(i, g)
-        for g in range(PASSES):
-            interleave(nc.scalar.copy, 0, g, 1)
-        for i in range(HEAD_TILES):
-            a_passes(i)
-            scale_ab(i)
-        for i in range(HEAD_TILES, LEAD):
-            ab(i)
-            g, step = divmod(i - HEAD_TILES, 2)
-            if g < PASSES:
-                if step == 0:
-                    interleave(nc.vector.tensor_copy, 0, g, 0)
-                else:
-                    quantize_c(0, g)
-
-        subtract_early(nc.vector, 0)
-        subtract_early(nc.gpsimd, 1)
-        subtract_early(nc.gpsimd, 2)
+        interleave(nc.scalar.copy, 0, 0, 1)
+        interleave(nc.scalar.copy, 0, 1, 1)
+        a_passes(0)
+        scale_ab(0)
+        a_passes(1)
+        scale_ab(1)
+        ab(2)
+        interleave(nc.vector.tensor_copy, 0, 0, 0)
+        ab(3)
+        quantize_c(0, 0)
+        ab(4)
+        interleave(nc.vector.tensor_copy, 0, 1, 0)
+        ab(5)
+        quantize_c(0, 1)
+        subtract_early(nc.vector, 0, "s0")
+        ab(6)
+        ab(7)
+        subtract_early(nc.gpsimd, 1, "shared")
+        subtract_early(nc.gpsimd, 2, "s2")
         finish_late(0)
         round_y(0)
         ab(8)
@@ -388,9 +391,9 @@ def tile_lazy_pruning_update_k3_kernel(
         ab(12)
         subtract_early(nc.gpsimd, 7)
         finish_late(5)
-        round_y(5)
-        subtract_early(nc.vector, 8)
+        subtract_early(nc.vector, 8, "spare")
         turn(0, 4, "xt")
+        round_y(5)
         finish_late(6)
         round_y(6)
         quantize_c(1, 1)
@@ -407,9 +410,9 @@ def tile_lazy_pruning_update_k3_kernel(
         subtract_early(nc.gpsimd, 11)
         interleave(nc.scalar.copy, 2, 0, 0)
         finish_late(9)
-        round_y(9)
-        subtract_early(nc.vector, 12)
         turn(4, 4, "xt")
+        round_y(9)
+        subtract_early(nc.gpsimd, 12)
         interleave(nc.scalar.copy, 2, 0, 1)
         finish_late(10)
         round_y(10)
@@ -430,9 +433,9 @@ def tile_lazy_pruning_update_k3_kernel(
         ab(18)
         subtract_early(nc.gpsimd, 15)
         finish_late(13)
-        round_y(13)
-        subtract_early(nc.vector, 16)
+        subtract_early(nc.vector, 16, s_slot[5])
         turn(8, 4, "xt")
+        round_y(13)
         finish_late(14)
         round_y(14)
         quantize_c(2, 1)
@@ -449,9 +452,9 @@ def tile_lazy_pruning_update_k3_kernel(
         ab(21)
         subtract_early(nc.gpsimd, 19)
         finish_late(17)
-        round_y(17)
-        subtract_early(nc.vector, 20)
         turn(12, 4, "xt")
+        round_y(17)
+        subtract_early(nc.gpsimd, 20)
         finish_late(18)
         round_y(18)
         ab(22)
@@ -463,20 +466,20 @@ def tile_lazy_pruning_update_k3_kernel(
         store_scales(1)
         ab(23)
         subtract_early(nc.gpsimd, 22)
-        subtract_early(nc.gpsimd, 23)
+        subtract_early(nc.gpsimd, 23, s_slot[13])
         turn(16, 2, "xt")
         finish_late(20)
         round_y(20)
         finish_late(21)
         round_y(21)
         turn(18, 2, "xt")
-        quantize_y(16, 0, 2)
         finish_late(22)
         round_y(22)
         finish_late(23)
         turn(20, 2, "ab")
         turn(22, 1, "ab")
         turn(23, 1, "ab")
+        quantize_y(16, 0, 2)
         quantize_y(18, 0, 2)
         store_codes(2, 0, 4)
         quantize_y(20, 0, 2)

@@ -25,7 +25,7 @@ PASSES = BLK // 512
 MTILES = ROWS // P
 NTILES = REST // NT
 WIDE = REST - NT
-F_CHUNKS = [(0, 2), (2, 5), (5, 8)]
+F_CHUNKS = [(0, 3), (3, 6), (6, 8)]
 V_FIRST = [(0, 2), (2, 4), (4, 6), (6, 8)]
 V_WIDE = [(0, 2), (2, 4), (4, 6), (6, 8)]
 HEAD_TILES = F_CHUNKS[0][1]
@@ -340,7 +340,7 @@ def tile_lazy_pruning_update_k3_kernel(
         for k in range(WARM):
             lhs, lhs_scale = f_operand(0, 0)
             nc.tensor.matmul_mx(
-                out=warm[:, : 2 * P], lhsT=lhs, lhsT_scale=lhs_scale, rhs=f_head[0][:].bitcast(FP8X4),
+                out=warm[:, : 2 * P], lhsT=lhs, lhsT_scale=lhs_scale, rhs=f_head[0][:, : 2 * P].bitcast(FP8X4),
                 rhs_scale=f_plane[:, 0, : 2 * P], start=True, stop=True,
             )
         for g in range(PASSES):
@@ -352,7 +352,8 @@ def tile_lazy_pruning_update_k3_kernel(
         scale_ab(0)
         a_passes(1)
         scale_ab(1)
-        ab(2)
+        a_passes(2)
+        scale_ab(2)
         interleave(nc.vector.tensor_copy, 0, 0, 0)
         ab(3)
         quantize_c(0, 0)

@@ -239,7 +239,7 @@ def tile_lazy_pruning_update_k3_kernel(
 
         def c_passes(j):
             m, n = TILES[j]
-            acc = bank("c")
+            acc = bank("ab" if j == len(TILES) - 1 else "c")
             for g in range(PASSES):
                 mm(acc, m, g, c_codes[n][g][:].bitcast(FP8X4), c_plane[n][g][:], g == 0, g == PASSES - 1)
             return acc
@@ -263,6 +263,15 @@ def tile_lazy_pruning_update_k3_kernel(
         def round_y(j):
             nc.scalar.copy(out=rounded(j), in_=word_order(y_done[j]))
 
+        def round_y_gpsimd(j):
+            nc.gpsimd.tensor_scalar(out=rounded(j), in0=word_order(y_done[j]), scalar1=1.0, scalar2=0.0, op0=MULT, op1=ADD)
+
+        def subtract_over(j, grp):
+            tile = TILES[j]
+            s = grp[:].rearrange("p m t -> p (m t)").bitcast(F32)[:, :NT]
+            nc.gpsimd.tensor_tensor(out=s, in0=v_of(tile), in1=part[tile][:], op=SUB)
+            part[tile] = s
+
         def subtract_early(engine, j, slot=None):
             tile = TILES[j]
             tag = s_slot[j] = slot or s_slot[j - S_AHEAD]
@@ -270,13 +279,39 @@ def tile_lazy_pruning_update_k3_kernel(
             engine.tensor_tensor(out=s[:], in0=v_of(tile), in1=part[tile][:], op=SUB)
             part[tile] = s
 
+        c_acc = {}
+
+        def direct_bf(j):
+            c_acc[j] = c_passes(j)
+            nc.vector.tensor_tensor(out=rounded(j), in0=word_order(part[TILES[j]][:]), in1=word_order(c_acc[j][:]), op=SUB)
+
+        def finish_halves(j):
+            m, n = TILES[j]
+            tile = TILES[j]
+            halves = [slice(0, NT // 2), slice(NT // 2, NT)]
+            accs = []
+            for cols in halves:
+                acc = bank("ab")[:, : NT // 2]
+                for g in range(PASSES):
+                    lhs, lhs_scale = f_operand(m, g)
+                    nc.tensor.matmul_mx(
+                        out=acc, lhsT=lhs, lhsT_scale=lhs_scale, rhs=c_codes[n][g][:, cols].bitcast(FP8X4),
+                        rhs_scale=c_plane[n][g][:, cols], start=g == 0, stop=g == PASSES - 1,
+                    )
+                accs.append(acc)
+            out_bf = rounded(j)
+            for h, (cols, acc) in enumerate(zip(halves, accs)):
+                words = out_bf[:, :, h * P // 2 : (h + 1) * P // 2, :]
+                nc.vector.tensor_tensor(out=words, in0=word_order(part[tile][:, cols]), in1=word_order(acc), op=SUB)
+            y = y_of(tile)
+            for cols, acc in zip(halves, accs):
+                nc.vector.tensor_tensor(out=y[:, cols], in0=part[tile][:, cols], in1=acc, op=SUB)
+            store_y(tile, y)
+
         def finish_late(j):
             tile = TILES[j]
-            acc = c_passes(j)
+            acc = c_acc[j] if j in c_acc else c_passes(j)
             y = y_of(tile)
-            last = j == len(TILES) - 1
-            if last:
-                nc.vector.tensor_tensor(out=rounded(j), in0=word_order(part[tile][:]), in1=word_order(acc[:]), op=SUB)
             nc.vector.tensor_tensor(out=y, in0=part[tile][:], in1=acc[:], op=SUB)
             store_y(tile, y)
             y_done[j] = y
@@ -299,13 +334,17 @@ def tile_lazy_pruning_update_k3_kernel(
                 in_=c_grp[n, g][:].rearrange("p w t -> p (w t)"),
             )
 
-        def turn(first, count, kind):
+        def empty(moves, engine_copy=nc.scalar.copy):
+            for dst, src in moves:
+                engine_copy(out=dst, in_=src)
+
+        def turn(first, count, kind, later=False):
             grp = work.tile([P, count * P, 4], BF16, name="y_grp", tag="y_grp", bufs=GRP_BUFS, align_bytes=64)
             y_grp[first] = grp
             grp_words = grp[:].rearrange("p m t -> p (m t)").bitcast(F32)
             banks = []
             for lo in range(0, count, 2):
-                xt = bank(kind)
+                xt = bank(kind if lo < 4 else "ab")
                 span = min(2, count - lo)
                 banks.append((xt, lo, span))
                 for s in range(span):
@@ -313,11 +352,16 @@ def tile_lazy_pruning_update_k3_kernel(
                     for u in range(2):
                         slot = 2 * s + u
                         nc.tensor.transpose(xt[:, P * slot : P * (slot + 1)], words[:, P * u : P * (u + 1)], ident[:])
-            for xt, lo, span in banks:
-                nc.scalar.copy(
-                    out=grp_words[:, 2 * P * lo : 2 * P * (lo + span)].rearrange("p (s r u) -> p s r u", r=P, u=2),
-                    in_=xt[:, : 2 * P * span].rearrange("p (s u r) -> p s r u", r=P, u=2),
+            moves = [
+                (
+                    grp_words[:, 2 * P * lo : 2 * P * (lo + span)].rearrange("p (s r u) -> p s r u", r=P, u=2),
+                    xt[:, : 2 * P * span].rearrange("p (s u r) -> p s r u", r=P, u=2),
                 )
+                for xt, lo, span in banks
+            ]
+            if later:
+                return moves
+            empty(moves)
 
         def quantize_y(first, lo, count):
             m, n = TILES[first + lo]
@@ -332,8 +376,8 @@ def tile_lazy_pruning_update_k3_kernel(
             move(nc.sync, out_1[n].rearrange("p m t -> p (m t)")[:, 4 * P * lo : 4 * P * hi], y_codes[n][:, P * lo : P * hi])
 
         def store_scales(n):
-            for q in range(4):
-                move(nc.scalar if n == NTILES - 1 and q % 2 else nc.sync, out_2[n, 4 * q : 4 * q + 4, :], y_plane[n][QUAD * q : QUAD * q + 4, :])
+            for r in range(4):
+                move(nc.scalar if n == NTILES - 1 and r % 2 else nc.sync, out_2[n, r::4, :], y_plane[n][r:P:QUAD, :])
 
         spread_d()
         warm = bank("c")
@@ -414,12 +458,11 @@ def tile_lazy_pruning_update_k3_kernel(
         turn(4, 4, "xt")
         round_y(9)
         subtract_early(nc.gpsimd, 12)
-        interleave(nc.scalar.copy, 2, 0, 1)
         finish_late(10)
         round_y(10)
         ab(16)
         subtract_early(nc.gpsimd, 13)
-        interleave(nc.scalar.copy, 2, 1, 0)
+        interleave(nc.scalar.copy, 2, 0, 1)
         finish_late(11)
         round_y(11)
         quantize_y(4, 0, 4)
@@ -427,12 +470,13 @@ def tile_lazy_pruning_update_k3_kernel(
         store_scales(0)
         ab(17)
         subtract_early(nc.gpsimd, 14)
-        interleave(nc.scalar.copy, 2, 1, 1)
+        interleave(nc.scalar.copy, 2, 1, 0)
         finish_late(12)
         round_y(12)
         quantize_c(2, 0)
         ab(18)
         subtract_early(nc.gpsimd, 15)
+        interleave(nc.scalar.copy, 2, 1, 1)
         finish_late(13)
         subtract_early(nc.vector, 16, s_slot[5])
         turn(8, 4, "xt")
@@ -468,24 +512,24 @@ def tile_lazy_pruning_update_k3_kernel(
         ab(23)
         subtract_early(nc.gpsimd, 22)
         subtract_early(nc.gpsimd, 23, s_slot[13])
-        turn(16, 2, "xt")
         finish_late(20)
         round_y(20)
         finish_late(21)
         round_y(21)
-        turn(18, 2, "xt")
         finish_late(22)
+        mv = turn(16, 4, "xt", True)
         round_y(22)
-        finish_late(23)
-        turn(20, 2, "ab")
-        turn(22, 1, "ab")
-        turn(23, 1, "ab")
-        quantize_y(16, 0, 2)
-        quantize_y(18, 0, 2)
+        empty(mv[:1], nc.vector.tensor_copy)
+        empty(mv[1:])
+        finish_halves(23)
+        turn(20, 2, "c")
+        turn(22, 1, "c")
+        turn(23, 1, "c")
+        quantize_y(16, 0, 4)
         store_codes(2, 0, 4)
         quantize_y(20, 0, 2)
-        store_codes(2, 4, 6)
         quantize_y(22, 0, 1)
+        store_codes(2, 4, 7)
         quantize_y(23, 0, 1)
-        store_codes(2, 6, 8)
+        store_codes(2, 7, 8)
         store_scales(2)

@@ -20,28 +20,27 @@ EQUAL = mybir.AluOpType.is_equal
 P = 128
 NT = 512
 QUAD = 32
-D_WORDS = REST // P // 2
 PASSES = BLK // 512
 MTILES = ROWS // P
-NTILES = REST // NT
+RANGES = REST // NT
+TILES = MTILES * RANGES
 WIDE = REST - NT
+D_WORDS = REST // P // 2
 F_CHUNKS = [(0, 3), (3, 6), (6, 8)]
-V_FIRST = [(0, 2), (2, 4), (4, 6), (6, 8)]
-V_WIDE = [(0, 2), (2, 4), (4, 6), (6, 8)]
 HEAD_TILES = F_CHUNKS[0][1]
+V_ROWS = 2
+B_ROW = 4
 LEAD = MTILES
 GROUP = 4
+FIRST_RUN = GROUP + 1
+LAST_ROUNDS = 4
+S_AHEAD = 3
 WARM = 4
-B_ROW = 4
-PART_BUFS = 9
+T_BUFS = LEAD + 1
 Y_BUFS = 12
-BF_BUFS = 8
+BF_BUFS = 2 * GROUP
 GRP_BUFS = 6
 C_BUFS = 3
-S_AHEAD = 3
-
-TILES = [(m, n) for n in range(NTILES) for m in range(MTILES)]
-AB_TILES = TILES
 
 
 def tile_lazy_pruning_update_k3_kernel(
@@ -62,24 +61,26 @@ def tile_lazy_pruning_update_k3_kernel(
         b_first = kept("b_first", [P, PASSES, NT], U8)
         ab_rest = kept("ab_rest", [P, PASSES, WIDE], U8)
         f_head = [kept("f_head%d" % g, [P, HEAD_TILES * P], U32) for g in range(PASSES)]
-        f_codes = [kept("f_codes%d" % lo, [P, PASSES, (hi - lo) * P], U32) if lo else None for lo, hi in F_CHUNKS]
-        a_codes = [kept("a_codes%d" % n, [P, PASSES, 2 * NT], U8) for n in range(NTILES)]
+        f_codes = {lo: kept("f_codes%d" % lo, [P, PASSES, (hi - lo) * P], U32) for lo, hi in F_CHUNKS[1:]}
+        a_codes = [kept("a_codes%d" % n, [P, PASSES, 2 * NT], U8) for n in range(RANGES)]
         b_head = [kept("b_head%d" % g, [P, NT], U32) for g in range(PASSES)]
-        b_codes = [kept("b_codes%d" % n, [P, PASSES, NT], U32) if n else None for n in range(NTILES)]
-        c_raw = [[kept("c_raw%d_%d" % (n, g), [P, 4, NT], BF16) for g in range(PASSES)] for n in range(NTILES)]
-        c_codes = [[kept("c_codes%d_%d" % (n, g), [P, NT], U32) for g in range(PASSES)] for n in range(NTILES)]
-        c_plane = [[kept("c_plane%d_%d" % (n, g), [P, NT], U8) for g in range(PASSES)] for n in range(NTILES)]
-        v_first = [kept("v_first%d" % lo, [P, hi - lo, NT], BF16) for lo, hi in V_FIRST]
-        v_wide = [kept("v_wide%d" % lo, [P, hi - lo, WIDE], BF16) for lo, hi in V_WIDE]
+        b_codes = {n: kept("b_codes%d" % n, [P, PASSES, NT], U32) for n in range(1, RANGES)}
+        c_raw = [[kept("c_raw%d_%d" % (n, g), [P, 4, NT], BF16) for g in range(PASSES)] for n in range(RANGES)]
+        c_codes = [[kept("c_codes%d_%d" % (n, g), [P, NT], U32) for g in range(PASSES)] for n in range(RANGES)]
+        c_plane = [[kept("c_plane%d_%d" % (n, g), [P, NT], U8) for g in range(PASSES)] for n in range(RANGES)]
+        v_first = [kept("v_first%d" % h, [P, V_ROWS, NT], BF16) for h in range(MTILES // V_ROWS)]
+        v_wide = [kept("v_wide%d" % h, [P, V_ROWS, WIDE], BF16) for h in range(MTILES // V_ROWS)]
         d_col = kept("d_col", [P, REST // P], BF16)
-        d_row = kept("d_row", [P, NTILES, NT], BF16)
+        d_row = kept("d_row", [P, RANGES, NT], BF16)
         ident = kept("ident", [P, P], F32)
-        y_codes = [kept("y_codes%d" % n, [P, ROWS], U32) for n in range(NTILES)]
-        y_plane = [kept("y_plane%d" % n, [P, ROWS], U8) for n in range(NTILES)]
+        y_codes = [kept("y_codes%d" % n, [P, ROWS], U32) for n in range(RANGES)]
+        y_plane = [kept("y_plane%d" % n, [P, ROWS], U8) for n in range(RANGES)]
 
         f_view = f_words.rearrange("g p m t -> p g (m t)")
         a_view = a_words.rearrange("g p x -> p g x")
         b_view = b_words.rearrange("g p n t -> p g (n t)")
+        first_cols, wide_cols = slice(0, NT), slice(NT, REST)
+
 
         def move(queue, dst, src):
             queue.dma_start(out=dst.bitcast(I32), in_=src.bitcast(I32))
@@ -89,9 +90,9 @@ def tile_lazy_pruning_update_k3_kernel(
                 lo = QUAD * q + first_row
                 move(queue, plane[lo : lo + 4, :, :], scales[:, 4 * q : 4 * q + 4, :].rearrange("g r n -> r g n"))
 
-        def load_f(k):
-            lo, hi = F_CHUNKS[k]
-            move(nc.sync, f_codes[k][:], f_view[:, :, 4 * P * lo : 4 * P * hi])
+        def load_f(chunk):
+            lo, hi = F_CHUNKS[chunk]
+            move(nc.sync, f_codes[lo][:], f_view[:, :, 4 * P * lo : 4 * P * hi])
 
         def load_a(queue, n):
             move(queue, a_codes[n][:], a_view[:, :, 2 * NT * n : 2 * NT * (n + 1)])
@@ -103,8 +104,12 @@ def tile_lazy_pruning_update_k3_kernel(
             rows = c[512 * g : 512 * (g + 1), NT * n : NT * (n + 1)]
             nc.sync.dma_start(out=c_raw[n][g][:], in_=rows.rearrange("(p j) w -> p j w", j=4))
 
-        def load_v(tile, tiles, cols):
-            nc.sync.dma_start(out=tile[:], in_=v[P * tiles[0] : P * tiles[1], cols].rearrange("(m p) w -> p m w", p=P))
+        def load_v(tiles, h, cols):
+            rows = v[P * V_ROWS * h : P * V_ROWS * (h + 1), cols]
+            nc.sync.dma_start(out=tiles[h][:], in_=rows.rearrange("(m p) w -> p m w", p=P))
+
+        def zero(plane):
+            nc.vector.memset(plane[:].rearrange("p g n -> p (g n)").bitcast(I32), 0)
 
         def build_identity():
             ones = kept("ones", [P, QUAD], F32)
@@ -118,11 +123,6 @@ def tile_lazy_pruning_update_k3_kernel(
                 rows = slice(QUAD * q, QUAD * (q + 1))
                 nc.vector.tensor_tensor(out=ident[rows, rows], in0=ramp[rows, :], in1=ramp_turned[rows, :], op=EQUAL)
 
-        def zero(plane):
-            nc.vector.memset(plane[:].rearrange("p g n -> p (g n)").bitcast(I32), 0)
-
-        first_cols, wide_cols = slice(0, NT), slice(NT, REST)
-
         move(nc.gpsimd, b_head[0][:], b_view[:, 0, : 4 * NT])
         load_a(nc.gpsimd, 0)
         zero(f_plane)
@@ -131,6 +131,7 @@ def tile_lazy_pruning_update_k3_kernel(
         zero(a_first)
         zero(ab_rest)
         load_scales(nc.gpsimd, ab_rest, b_scales[:, :, wide_cols], B_ROW)
+
         nc.sync.dma_start(out=d_col[:], in_=d.rearrange("(p j) -> p j", p=P))
         move(nc.sync, f_head[0][:], f_view[:, 0, : 4 * P * HEAD_TILES])
         load_scales(nc.sync, f_plane, f_scales, 0)
@@ -138,398 +139,267 @@ def tile_lazy_pruning_update_k3_kernel(
         move(nc.sync, f_head[1][:], f_view[:, 1, : 4 * P * HEAD_TILES])
         move(nc.sync, b_head[1][:], b_view[:, 1, : 4 * NT])
         load_scales(nc.sync, a_first, a_scales[:, :, first_cols], 0)
-        load_f(1)
-        load_c(0, 0)
-        load_f(2)
-        load_c(0, 1)
+        for g in range(PASSES):
+            load_f(1 + g)
+            load_c(0, g)
         load_scales(nc.sync, ab_rest, a_scales[:, :, wide_cols], 0)
-        load_v(v_first[0], V_FIRST[0], first_cols)
+        load_v(v_first, 0, first_cols)
         load_b(1)
         load_a(nc.sync, 1)
-        load_v(v_first[1], V_FIRST[1], first_cols)
+        load_v(v_first, 1, first_cols)
         load_c(1, 0)
-        load_v(v_first[2], V_FIRST[2], first_cols)
-        load_v(v_first[3], V_FIRST[3], first_cols)
+        load_v(v_first, 2, first_cols)
+        load_v(v_first, 3, first_cols)
         load_c(1, 1)
-        load_v(v_wide[0], V_WIDE[0], wide_cols)
-        load_v(v_wide[1], V_WIDE[1], wide_cols)
+        load_v(v_wide, 0, wide_cols)
+        load_v(v_wide, 1, wide_cols)
         load_b(2)
         load_a(nc.sync, 2)
-        load_c(2, 0)
-        load_v(v_wide[2], V_WIDE[2], wide_cols)
-        load_c(2, 1)
-        load_v(v_wide[3], V_WIDE[3], wide_cols)
+        for g in range(PASSES):
+            load_c(2, g)
+            load_v(v_wide, 2 + g, wide_cols)
+
 
         def bank(kind):
-            bufs = {"ab": 3, "c": 3, "xt": 2}[kind]
-            return psum.tile([P, NT], F32, name=kind, tag=kind, bufs=bufs)
+            return psum.tile([P, NT], F32, name=kind, tag=kind, bufs={"ab": 3, "c": 3, "xt": 2}[kind])
 
         def spread_d():
             d_words = d_col[:].bitcast(F32)
             d_row_words = d_row[:].rearrange("r n w -> r (n w)").bitcast(F32).rearrange("r (p w) -> r p w", p=P)
-            for lo, hi in ((0, 4), (4, D_WORDS)):
+            for lo, hi in ((0, NT // P), (NT // P, D_WORDS)):
                 xt = bank("xt")
                 for w in range(lo, hi):
                     slot = slice(P * (w - lo), P * (w - lo + 1))
                     nc.tensor.transpose(xt[:, slot], d_words[:, w : w + 1].to_broadcast([P, P]), ident[:])
                 nc.scalar.copy(out=d_row_words[:, :, lo:hi], in_=xt[:, : P * (hi - lo)].rearrange("r (w p) -> r p w", p=P))
 
-        def chunk_of(chunks, m):
-            k = [lo <= m < hi for lo, hi in chunks].index(True)
-            return k, m - chunks[k][0]
-
-        def f_operand(m, g):
-            k, off = chunk_of(F_CHUNKS, m)
-            cols = slice(P * off, P * (off + 1))
-            codes = f_codes[k][:, g, cols] if k else f_head[g][:, cols]
-            return codes.bitcast(FP8X4), f_plane[:, g, P * m : P * (m + 1)]
-
         def mm(acc, m, g, rhs, rhs_scale, start, stop):
-            lhs, lhs_scale = f_operand(m, g)
+            lo = max(first for first, end in F_CHUNKS if first <= m)
+            cols = slice(P * (m - lo), P * (m - lo + 1))
+            codes = f_codes[lo][:, g, cols] if lo else f_head[g][:, cols]
             nc.tensor.matmul_mx(
-                out=acc[:], lhsT=lhs, lhsT_scale=lhs_scale, rhs=rhs, rhs_scale=rhs_scale, start=start, stop=stop
+                out=acc, lhsT=codes.bitcast(FP8X4), lhsT_scale=f_plane[:, g, P * m : P * (m + 1)],
+                rhs=rhs, rhs_scale=rhs_scale, start=start, stop=stop,
             )
 
-        s_slot = {}
-        ab_acc, part, y_bf, y_grp, c_grp, y_done = {}, {}, {}, {}, {}, {}
+        ab_acc, t_of, s_of, s_tag, y_of, y_bf, y_grp, c_grp = {}, {}, {}, {}, {}, {}, {}, {}
 
         def plane_of(first, n, g, row):
             return first[row:P, g, :] if n == 0 else ab_rest[row:P, g, NT * (n - 1) : NT * n]
 
         def b_pass(i, g):
-            m, n = AB_TILES[i]
+            n, m = divmod(i, MTILES)
             if g == 0:
-                ab_acc[i] = bank("c" if 3 <= i < 6 else "ab")
+                ab_acc[i] = bank("c" if HEAD_TILES <= i < 2 * HEAD_TILES else "ab")
             codes = b_codes[n][:, g, :] if n else b_head[g][:]
-            mm(ab_acc[i], m, g, codes.bitcast(FP8X4), plane_of(b_first, n, g, B_ROW), g == 0, False)
+            mm(ab_acc[i][:], m, g, codes.bitcast(FP8X4), plane_of(b_first, n, g, B_ROW), g == 0, False)
 
-        def a_passes(i):
-            m, n = AB_TILES[i]
+        def a_passes_and_t(i):
+            n, m = divmod(i, MTILES)
             for g in range(PASSES):
-                mm(ab_acc[i], m, g, a_codes[n][:, g, :].bitcast(FP4X4), plane_of(a_first, n, g, 0), False, g == PASSES - 1)
+                mm(ab_acc[i][:], m, g, a_codes[n][:, g, :].bitcast(FP4X4), plane_of(a_first, n, g, 0), False, g == PASSES - 1)
+            t_of[i] = work.tile([P, NT], F32, name="t", tag="t", bufs=T_BUFS)
+            nc.vector.tensor_tensor(out=t_of[i][:], in0=d_row[:, n, :], in1=ab_acc[i][:], op=MULT)
 
-        def scale_ab(i):
-            tile = AB_TILES[i]
-            part[tile] = work.tile([P, NT], F32, name="part", tag="part", bufs=PART_BUFS)
-            nc.vector.tensor_tensor(out=part[tile][:], in0=d_row[:, tile[1], :], in1=ab_acc[i][:], op=MULT)
-
-        def ab(i):
+        def ab_group(i):
             for g in range(PASSES):
                 b_pass(i, g)
-            a_passes(i)
-            scale_ab(i)
+            a_passes_and_t(i)
 
-        def v_of(tile):
-            m, n = tile
-            if n == 0:
-                k, off = chunk_of(V_FIRST, m)
-                return v_first[k][:, off, :]
-            k, off = chunk_of(V_WIDE, m)
-            return v_wide[k][:, off, NT * (n - 1) : NT * n]
+        def subtract(engine, j, tag):
+            n, m = divmod(j, MTILES)
+            h, row = divmod(m, V_ROWS)
+            v_tile = v_wide[h][:, row, NT * (n - 1) : NT * n] if n else v_first[h][:, row, :]
+            s_tag[j] = tag
+            s_of[j] = work.tile([P, NT], F32, name=tag, tag=tag, bufs=1, align_bytes=64)
+            engine.tensor_tensor(out=s_of[j][:], in0=v_tile, in1=t_of[j][:], op=SUB)
 
-        def y_of(tile):
-            return work.tile([P, NT], F32, name="y", tag="y", bufs=Y_BUFS)[:]
+        def c_group(j, kind, cols):
+            n, m = divmod(j, MTILES)
+            acc = bank(kind)[:, : cols.stop - cols.start]
+            for g in range(PASSES):
+                mm(acc, m, g, c_codes[n][g][:, cols].bitcast(FP8X4), c_plane[n][g][:, cols], g == 0, g == PASSES - 1)
+            return acc
 
-        def store_y(tile, y):
-            m, n = tile
-            nc.sync.dma_start(out=out_0[P * m : P * (m + 1), NT * n : NT * (n + 1)], in_=y)
+        def form_y(j, parts):
+            n, m = divmod(j, MTILES)
+            y_of[j] = work.tile([P, NT], F32, name="y", tag="y", bufs=Y_BUFS)
+            for cols, acc in parts:
+                nc.vector.tensor_tensor(out=y_of[j][:, cols], in0=s_of[j][:, cols], in1=acc, op=SUB)
+            nc.sync.dma_start(out=out_0[P * m : P * (m + 1), NT * n : NT * (n + 1)], in_=y_of[j][:])
+
+        def finish(j):
+            form_y(j, [(first_cols, c_group(j, "c", first_cols))])
 
         def word_order(ap):
             return ap.rearrange("r (p u e) -> r u p e", u=2, e=2)
 
-        def c_passes(j):
-            m, n = TILES[j]
-            acc = bank("ab" if j == len(TILES) - 1 else "c")
-            for g in range(PASSES):
-                mm(acc, m, g, c_codes[n][g][:].bitcast(FP8X4), c_plane[n][g][:], g == 0, g == PASSES - 1)
-            return acc
-
-        def rounded(j):
+        def new_rounded(j):
             y_bf[j] = work.tile([P, 2, P, 2], BF16, name="y_bf", tag="y_bf", bufs=BF_BUFS, align_bytes=64)
             return y_bf[j][:]
 
-        def add_c(j):
-            tile = TILES[j]
-            acc = c_passes(j)
-            nc.vector.tensor_tensor(out=part[tile][:], in0=part[tile][:], in1=acc[:], op=ADD)
-
-        def finish(engine, j):
-            tile = TILES[j]
-            y = y_of(tile)
-            engine.tensor_tensor(out=y, in0=v_of(tile), in1=part[tile][:], op=SUB)
-            store_y(tile, y)
-            y_done[j] = y
-
         def round_y(j):
-            nc.scalar.copy(out=rounded(j), in_=word_order(y_done[j]))
+            nc.scalar.copy(out=new_rounded(j), in_=word_order(y_of[j][:]))
 
-        def round_y_gpsimd(j):
-            nc.gpsimd.tensor_scalar(out=rounded(j), in0=word_order(y_done[j]), scalar1=1.0, scalar2=0.0, op0=MULT, op1=ADD)
-
-        def subtract_over(j, grp):
-            tile = TILES[j]
-            s = grp[:].rearrange("p m t -> p (m t)").bitcast(F32)[:, :NT]
-            nc.gpsimd.tensor_tensor(out=s, in0=v_of(tile), in1=part[tile][:], op=SUB)
-            part[tile] = s
-
-        def subtract_early(engine, j, slot=None):
-            tile = TILES[j]
-            tag = s_slot[j] = slot or s_slot[j - S_AHEAD]
-            s = work.tile([P, NT], F32, name=tag, tag=tag, bufs=1, align_bytes=64)
-            engine.tensor_tensor(out=s[:], in0=v_of(tile), in1=part[tile][:], op=SUB)
-            part[tile] = s
-
-        c_acc = {}
-
-        def direct_bf(j):
-            c_acc[j] = c_passes(j)
-            nc.vector.tensor_tensor(out=rounded(j), in0=word_order(part[TILES[j]][:]), in1=word_order(c_acc[j][:]), op=SUB)
-
-        def finish_halves(j):
-            m, n = TILES[j]
-            tile = TILES[j]
+        def finish_last(j):
             halves = [slice(0, NT // 2), slice(NT // 2, NT)]
-            accs = []
-            for cols in halves:
-                acc = bank("ab")[:, : NT // 2]
-                for g in range(PASSES):
-                    lhs, lhs_scale = f_operand(m, g)
-                    nc.tensor.matmul_mx(
-                        out=acc, lhsT=lhs, lhsT_scale=lhs_scale, rhs=c_codes[n][g][:, cols].bitcast(FP8X4),
-                        rhs_scale=c_plane[n][g][:, cols], start=g == 0, stop=g == PASSES - 1,
-                    )
-                accs.append(acc)
-            out_bf = rounded(j)
-            for h, (cols, acc) in enumerate(zip(halves, accs)):
-                words = out_bf[:, :, h * P // 2 : (h + 1) * P // 2, :]
-                nc.vector.tensor_tensor(out=words, in0=word_order(part[tile][:, cols]), in1=word_order(acc), op=SUB)
-            y = y_of(tile)
-            for cols, acc in zip(halves, accs):
-                nc.vector.tensor_tensor(out=y[:, cols], in0=part[tile][:, cols], in1=acc, op=SUB)
-            store_y(tile, y)
-
-        def finish_late(j):
-            tile = TILES[j]
-            acc = c_acc[j] if j in c_acc else c_passes(j)
-            y = y_of(tile)
-            nc.vector.tensor_tensor(out=y, in0=part[tile][:], in1=acc[:], op=SUB)
-            store_y(tile, y)
-            y_done[j] = y
+            parts = [(cols, c_group(j, "ab", cols)) for cols in halves]
+            rounded = new_rounded(j)
+            for h, (cols, acc) in enumerate(parts):
+                words = rounded[:, :, h * P // 2 : (h + 1) * P // 2, :]
+                nc.vector.tensor_tensor(out=words, in0=word_order(s_of[j][:, cols]), in1=word_order(acc), op=SUB)
+            form_y(j, parts)
 
         def interleave(engine_copy, n, g, h):
             if (n, g) not in c_grp:
-                tag, bufs = ("shared", 1) if (n, g) == (0, PASSES - 1) else ("c_grp", C_BUFS)
+                tag, bufs = ("handed_on", 1) if (n, g) == (0, PASSES - 1) else ("c_grp", C_BUFS)
                 c_grp[n, g] = work.tile([P, NT, 4], BF16, name="c_grp", tag=tag, bufs=bufs, align_bytes=64)
-            raw = c_raw[n][g]
             cols = slice(h * NT // 2, (h + 1) * NT // 2)
             engine_copy(
                 out=c_grp[n, g][:, cols, :].rearrange("p (c i) t -> p c t i", i=4),
-                in_=raw[:, :, cols].rearrange("p t (c i) -> p c t i", i=4),
+                in_=c_raw[n][g][:, :, cols].rearrange("p t (c i) -> p c t i", i=4),
             )
 
         def quantize_c(n, g):
             nc.vector.quantize_mx(
-                out=c_codes[n][g][:].bitcast(FP8X4),
-                scales=c_plane[n][g][:],
-                in_=c_grp[n, g][:].rearrange("p w t -> p (w t)"),
+                out=c_codes[n][g][:].bitcast(FP8X4), scales=c_plane[n][g][:], in_=c_grp[n, g][:].rearrange("p w t -> p (w t)")
             )
 
-        def empty(moves, engine_copy=nc.scalar.copy):
-            for dst, src in moves:
-                engine_copy(out=dst, in_=src)
-
-        def turn(first, count, kind, later=False):
-            grp = work.tile([P, count * P, 4], BF16, name="y_grp", tag="y_grp", bufs=GRP_BUFS, align_bytes=64)
-            y_grp[first] = grp
-            grp_words = grp[:].rearrange("p m t -> p (m t)").bitcast(F32)
-            banks = []
+        def turn(first, count, kind):
+            y_grp[first] = work.tile([P, count * P, 4], BF16, name="y_grp", tag="y_grp", bufs=GRP_BUFS, align_bytes=64)
+            grp_words = y_grp[first][:].rearrange("p m t -> p (m t)").bitcast(F32)
+            copies = []
             for lo in range(0, count, 2):
-                xt = bank(kind if lo < 4 else "ab")
+                xt = bank(kind)
                 span = min(2, count - lo)
-                banks.append((xt, lo, span))
                 for s in range(span):
                     words = y_bf[first + lo + s][:].rearrange("r u p e -> r (u p e)").bitcast(F32)
                     for u in range(2):
                         slot = 2 * s + u
                         nc.tensor.transpose(xt[:, P * slot : P * (slot + 1)], words[:, P * u : P * (u + 1)], ident[:])
-            moves = [
-                (
+                copies.append((
                     grp_words[:, 2 * P * lo : 2 * P * (lo + span)].rearrange("p (s r u) -> p s r u", r=P, u=2),
                     xt[:, : 2 * P * span].rearrange("p (s u r) -> p s r u", r=P, u=2),
-                )
-                for xt, lo, span in banks
-            ]
-            if later:
-                return moves
-            empty(moves)
+                ))
+            return copies
 
-        def quantize_y(first, lo, count):
-            m, n = TILES[first + lo]
+        def empty(engine_copy, copies):
+            for dst, src in copies:
+                engine_copy(out=dst, in_=src)
+
+        def quantize_y(first, count):
+            n, m = divmod(first, MTILES)
             cols = slice(P * m, P * (m + count))
             nc.vector.quantize_mx(
-                out=y_codes[n][:, cols].bitcast(FP8X4),
-                scales=y_plane[n][:, cols],
-                in_=y_grp[first][:, P * lo : P * (lo + count), :].rearrange("p m t -> p (m t)"),
+                out=y_codes[n][:, cols].bitcast(FP8X4), scales=y_plane[n][:, cols],
+                in_=y_grp[first][:].rearrange("p m t -> p (m t)"),
             )
 
         def store_codes(n, lo, hi):
             move(nc.sync, out_1[n].rearrange("p m t -> p (m t)")[:, 4 * P * lo : 4 * P * hi], y_codes[n][:, P * lo : P * hi])
 
-        def store_scales(n):
+        def store_scales(n, queues):
             for r in range(4):
-                move(nc.scalar if n == NTILES - 1 and r % 2 else nc.sync, out_2[n, r::4, :], y_plane[n][r:P:QUAD, :])
+                move(queues[r % len(queues)], out_2[n, r::4, :], y_plane[n][r:P:QUAD, :])
+
 
         spread_d()
         warm = bank("c")
         for k in range(WARM):
-            lhs, lhs_scale = f_operand(0, 0)
-            nc.tensor.matmul_mx(
-                out=warm[:, : 2 * P], lhsT=lhs, lhsT_scale=lhs_scale, rhs=f_head[0][:, : 2 * P].bitcast(FP8X4),
-                rhs_scale=f_plane[:, 0, : 2 * P], start=True, stop=True,
-            )
+            mm(warm[:, : 2 * P], 0, 0, f_head[0][:, : 2 * P].bitcast(FP8X4), f_plane[:, 0, : 2 * P], True, True)
         for g in range(PASSES):
             for i in range(HEAD_TILES):
                 b_pass(i, g)
-        interleave(nc.scalar.copy, 0, 0, 1)
-        interleave(nc.scalar.copy, 0, 1, 1)
-        a_passes(0)
-        scale_ab(0)
-        a_passes(1)
-        scale_ab(1)
-        a_passes(2)
-        scale_ab(2)
+        for g in range(PASSES):
+            interleave(nc.scalar.copy, 0, g, 1)
+        for i in range(HEAD_TILES):
+            a_passes_and_t(i)
         interleave(nc.vector.tensor_copy, 0, 0, 0)
-        ab(3)
+        ab_group(HEAD_TILES)
         quantize_c(0, 0)
-        ab(4)
+        ab_group(HEAD_TILES + 1)
         interleave(nc.vector.tensor_copy, 0, 1, 0)
-        ab(5)
+        ab_group(HEAD_TILES + 2)
         quantize_c(0, 1)
-        subtract_early(nc.vector, 0, "s0")
-        ab(6)
-        ab(7)
-        subtract_early(nc.gpsimd, 1, "shared")
-        subtract_early(nc.gpsimd, 2, "s2")
-        finish_late(0)
-        round_y(0)
-        ab(8)
-        subtract_early(nc.gpsimd, 3)
-        interleave(nc.scalar.copy, 1, 0, 0)
-        finish_late(1)
-        round_y(1)
-        ab(9)
-        subtract_early(nc.gpsimd, 4)
-        interleave(nc.scalar.copy, 1, 0, 1)
-        finish_late(2)
-        round_y(2)
-        ab(10)
-        subtract_early(nc.gpsimd, 5)
-        interleave(nc.scalar.copy, 1, 1, 0)
-        finish_late(3)
-        round_y(3)
-        ab(11)
-        subtract_early(nc.gpsimd, 6)
-        interleave(nc.scalar.copy, 1, 1, 1)
-        finish_late(4)
-        round_y(4)
-        quantize_c(1, 0)
-        ab(12)
-        subtract_early(nc.gpsimd, 7)
-        finish_late(5)
-        subtract_early(nc.vector, 8, "spare")
-        turn(0, 4, "xt")
-        round_y(5)
-        finish_late(6)
-        round_y(6)
-        quantize_c(1, 1)
-        ab(13)
-        subtract_early(nc.gpsimd, 9)
-        finish_late(7)
-        round_y(7)
-        quantize_y(0, 0, 4)
-        ab(14)
-        subtract_early(nc.gpsimd, 10)
-        finish_late(8)
-        round_y(8)
-        ab(15)
-        subtract_early(nc.gpsimd, 11)
-        interleave(nc.scalar.copy, 2, 0, 0)
-        finish_late(9)
-        turn(4, 4, "xt")
-        round_y(9)
-        subtract_early(nc.gpsimd, 12)
-        finish_late(10)
-        round_y(10)
-        ab(16)
-        subtract_early(nc.gpsimd, 13)
-        interleave(nc.scalar.copy, 2, 0, 1)
-        finish_late(11)
-        round_y(11)
-        quantize_y(4, 0, 4)
-        store_codes(0, 0, 8)
-        store_scales(0)
-        ab(17)
-        subtract_early(nc.gpsimd, 14)
-        interleave(nc.scalar.copy, 2, 1, 0)
-        finish_late(12)
-        round_y(12)
-        quantize_c(2, 0)
-        ab(18)
-        subtract_early(nc.gpsimd, 15)
-        interleave(nc.scalar.copy, 2, 1, 1)
-        finish_late(13)
-        subtract_early(nc.vector, 16, s_slot[5])
-        turn(8, 4, "xt")
-        round_y(13)
-        finish_late(14)
-        round_y(14)
-        quantize_c(2, 1)
-        ab(19)
-        subtract_early(nc.gpsimd, 17)
-        finish_late(15)
-        round_y(15)
-        quantize_y(8, 0, 4)
-        store_codes(1, 0, 4)
-        ab(20)
-        subtract_early(nc.gpsimd, 18)
-        finish_late(16)
-        round_y(16)
-        ab(21)
-        subtract_early(nc.gpsimd, 19)
-        finish_late(17)
-        turn(12, 4, "xt")
-        round_y(17)
-        subtract_early(nc.gpsimd, 20)
-        finish_late(18)
-        round_y(18)
-        ab(22)
-        subtract_early(nc.gpsimd, 21)
-        finish_late(19)
-        round_y(19)
-        quantize_y(12, 0, 4)
-        store_codes(1, 4, 8)
-        store_scales(1)
-        ab(23)
-        subtract_early(nc.gpsimd, 22)
-        subtract_early(nc.gpsimd, 23, s_slot[13])
-        finish_late(20)
-        round_y(20)
-        finish_late(21)
-        round_y(21)
-        finish_late(22)
-        mv = turn(16, 4, "xt", True)
-        round_y(22)
-        empty(mv[:1], nc.vector.tensor_copy)
-        empty(mv[1:])
-        finish_halves(23)
-        turn(20, 2, "c")
-        turn(22, 1, "c")
-        turn(23, 1, "c")
-        quantize_y(16, 0, 4)
-        store_codes(2, 0, 4)
-        quantize_y(20, 0, 2)
-        quantize_y(22, 0, 1)
-        store_codes(2, 4, 7)
-        quantize_y(23, 0, 1)
-        store_codes(2, 7, 8)
-        store_scales(2)
+        subtract(nc.vector, 0, "s_first")
+        for i in range(2 * HEAD_TILES, LEAD):
+            ab_group(i)
+        subtract(nc.gpsimd, 1, "handed_on")
+        subtract(nc.gpsimd, 2, "s_third")
+
+
+        rounds = TILES - LAST_ROUNDS
+        runs = {FIRST_RUN + first: first for first in range(0, rounds - FIRST_RUN, GROUP)}
+        y_jobs = {j + 2: first for j, first in runs.items()}
+        c_jobs = {MTILES * n - 4 + 2 * g: (n, g) for n in range(1, RANGES) for g in range(PASSES)}
+        halves = [(g, h) for g in range(PASSES) for h in range(2)]
+        late = [j for j in range(MTILES - 1, rounds) if j not in runs]
+        copy_jobs = {j: (1, g, h) for j, (g, h) in enumerate(halves)}
+        copy_jobs.update({j: (2, g, h) for j, (g, h) in zip(late, halves)})
+
+        idle = ["s_spare"]
+        next_ab, next_s = LEAD, S_AHEAD
+        for j in range(rounds):
+            finish(j)
+            fresh = s_tag[j]
+            quantises = j in c_jobs or j in y_jobs
+            if j not in runs:
+                round_y(j)
+            if j in c_jobs:
+                quantize_c(*c_jobs[j])
+            if j in y_jobs:
+                n, m = divmod(y_jobs[j], MTILES)
+                quantize_y(y_jobs[j], GROUP)
+                if n:
+                    store_codes(n, m, m + GROUP)
+                elif m:
+                    store_codes(n, 0, MTILES)
+                if m:
+                    store_scales(n, [nc.sync])
+            if j in runs:
+                subtract(nc.vector, next_s, idle.pop(0))
+                next_s += 1
+                empty(nc.scalar.copy, turn(runs[j], GROUP, "xt"))
+                round_y(j)
+                if j + 1 in c_jobs:
+                    idle.append(fresh)
+                else:
+                    subtract(nc.gpsimd, next_s, fresh)
+                    next_s += 1
+            else:
+                ab_group(next_ab)
+                next_ab += 1
+                if next_s > j + S_AHEAD:
+                    idle.append(fresh)
+                elif j + 1 in runs and not quantises:
+                    subtract(nc.gpsimd, next_s, idle.pop(0))
+                    idle.append(fresh)
+                    next_s += 1
+                else:
+                    subtract(nc.gpsimd, next_s, fresh)
+                    next_s += 1
+            if j in copy_jobs:
+                interleave(nc.scalar.copy, *copy_jobs[j])
+        subtract(nc.gpsimd, next_s, idle.pop(0))
+
+
+        last, n = TILES - 1, RANGES - 1
+        for j in range(rounds, last - 1):
+            finish(j)
+            round_y(j)
+        finish(last - 1)
+        copies = turn(rounds - GROUP, GROUP, "xt")
+        round_y(last - 1)
+        empty(nc.vector.tensor_copy, copies[:1])
+        empty(nc.scalar.copy, copies[1:])
+        finish_last(last)
+        for first, count in ((rounds, 2), (last - 1, 1), (last, 1)):
+            empty(nc.scalar.copy, turn(first, count, "c"))
+        quantize_y(rounds - GROUP, GROUP)
+        store_codes(n, 0, GROUP)
+        quantize_y(rounds, 2)
+        quantize_y(last - 1, 1)
+        store_codes(n, GROUP, MTILES - 1)
+        quantize_y(last, 1)
+        store_codes(n, MTILES - 1, MTILES)
+        store_scales(n, [nc.sync, nc.scalar])

@@ -299,8 +299,8 @@ def tile_lazy_pruning_update_k3_kernel(
             move(nc.sync, out_1[n].rearrange("p m t -> p (m t)")[:, 4 * P * lo : 4 * P * hi], y_codes[n][:, P * lo : P * hi])
 
         def store_scales(n, queues):
-            for r in range(4):
-                move(queues[r % len(queues)], out_2[n, r::4, :], y_plane[n][r:P:QUAD, :])
+            for q in range(4):
+                move(queues[q % len(queues)], out_2[n, 4 * q : 4 * q + 4, :], y_plane[n][QUAD * q : QUAD * q + 4, :])
 
 
         spread_d()

@@ -35,11 +35,12 @@ GROUP = 4
 FIRST_RUN = GROUP + 1
 LAST_ROUNDS = 4
 S_AHEAD = 3
+BLOCK_ROUND = MTILES - 1
 WARM = 4
 T_BUFS = LEAD + 1
-Y_BUFS = 12
+Y_BUFS = 16
 BF_BUFS = 2 * GROUP
-GRP_BUFS = 6
+GRP_BUFS = 5
 C_BUFS = 3
 
 
@@ -75,6 +76,9 @@ def tile_lazy_pruning_update_k3_kernel(
         ident = kept("ident", [P, P], F32)
         y_codes = [kept("y_codes%d" % n, [P, ROWS], U32) for n in range(RANGES)]
         y_plane = [kept("y_plane%d" % n, [P, ROWS], U8) for n in range(RANGES)]
+        blocks = kept("blocks", [P, GROUP, NT // 2], F32)
+        block_codes = kept("block_codes", [P, 4, GROUP * QUAD], U32)
+        block_plane = kept("block_plane", [P, GROUP * QUAD], U8)
 
         f_view = f_words.rearrange("g p m t -> p g (m t)")
         a_view = a_words.rearrange("g p x -> p g x")
@@ -283,6 +287,32 @@ def tile_lazy_pruning_update_k3_kernel(
                 ))
             return copies
 
+        def turn_blocks(j):
+            nc.vector.transpose(out=blocks[:, j, :], in_=y_bf[j][:].rearrange("r u p e -> r (u p e)").bitcast(F32))
+
+        def join_blocks():
+            y_grp[0] = work.tile([P, 4, GROUP * QUAD, 4], BF16, name="joined", tag="joined", bufs=1, align_bytes=64)
+            words = y_grp[0][:].rearrange("p b x t -> p (b x t)").bitcast(F32)
+            nc.scalar.copy(
+                out=words.rearrange("p (b m r u) -> p b m r u", b=4, m=GROUP, u=2),
+                in_=blocks[:].rearrange("p m (u b r) -> p b m r u", u=2, b=4),
+            )
+
+        def quantize_blocks():
+            for b in range(4):
+                nc.vector.quantize_mx(
+                    out=block_codes[:, b, :].bitcast(FP8X4), scales=block_plane[4 * b : P, :],
+                    in_=y_grp[0][:, b, :, :].rearrange("p x t -> p (x t)"),
+                )
+
+        def store_blocks(q):
+            codes = out_1[0, :, : GROUP * P, :].rearrange("p (m q r) t -> q p m (r t)", q=4, r=QUAD)
+            scales = out_2[0, :, : GROUP * P].rearrange("i (m q r) -> q i m r", q=4, r=QUAD)
+            for b in range(4):
+                src = block_codes[QUAD * q : QUAD * (q + 1), b, :].rearrange("p (m r) -> p m r", r=QUAD)
+                move(nc.sync, codes[q, QUAD * b : QUAD * (b + 1)], src)
+            move(nc.sync, scales[q], block_plane[QUAD * q : QUAD * q + 16, :].rearrange("i (m r) -> i m r", r=QUAD))
+
         def empty(engine_copy, copies):
             for dst, src in copies:
                 engine_copy(out=dst, in_=src)
@@ -298,9 +328,9 @@ def tile_lazy_pruning_update_k3_kernel(
         def store_codes(n, lo, hi):
             move(nc.sync, out_1[n].rearrange("p m t -> p (m t)")[:, 4 * P * lo : 4 * P * hi], y_codes[n][:, P * lo : P * hi])
 
-        def store_scales(n, queues):
+        def store_scales(n, lo):
             for q in range(4):
-                move(queues[q % len(queues)], out_2[n, 4 * q : 4 * q + 4, :], y_plane[n][QUAD * q : QUAD * q + 4, :])
+                move(nc.sync, out_2[n, 4 * q : 4 * q + 4, P * lo :], y_plane[n][QUAD * q : QUAD * q + 4, P * lo :])
 
 
         spread_d()
@@ -329,14 +359,15 @@ def tile_lazy_pruning_update_k3_kernel(
 
 
         rounds = TILES - LAST_ROUNDS
-        runs = {FIRST_RUN + first: first for first in range(0, rounds - FIRST_RUN, GROUP)}
-        y_jobs = {j + 2: first for j, first in runs.items()}
+        runs = {FIRST_RUN + first: first for first in range(GROUP, rounds - FIRST_RUN, GROUP)}
+        y_jobs = {j + (1 if j == max(runs) else 2): first for j, first in runs.items()}
         c_jobs = {MTILES * n - 4 + 2 * g: (n, g) for n in range(1, RANGES) for g in range(PASSES)}
         halves = [(g, h) for g in range(PASSES) for h in range(2)]
         late = [j for j in range(MTILES - 1, rounds) if j not in runs]
         copy_jobs = {j: (1, g, h) for j, (g, h) in enumerate(halves)}
         copy_jobs.update({j: (2, g, h) for j, (g, h) in zip(late, halves)})
 
+        block_turns = dict(zip([j for j in range(1, MTILES) if j not in c_jobs], range(GROUP)))
         idle = ["s_spare"]
         next_ab, next_s = LEAD, S_AHEAD
         for j in range(rounds):
@@ -350,12 +381,15 @@ def tile_lazy_pruning_update_k3_kernel(
             if j in y_jobs:
                 n, m = divmod(y_jobs[j], MTILES)
                 quantize_y(y_jobs[j], GROUP)
-                if n:
-                    store_codes(n, m, m + GROUP)
-                elif m:
-                    store_codes(n, 0, MTILES)
+                store_codes(n, m, m + GROUP)
                 if m:
-                    store_scales(n, [nc.sync])
+                    store_scales(n, 0 if n else GROUP)
+            if j in block_turns:
+                turn_blocks(block_turns[j])
+            if j == BLOCK_ROUND:
+                quantize_blocks()
+            if 0 <= j - BLOCK_ROUND < 4:
+                store_blocks(j - BLOCK_ROUND)
             if j in runs:
                 subtract(nc.vector, next_s, idle.pop(0))
                 next_s += 1
@@ -367,9 +401,17 @@ def tile_lazy_pruning_update_k3_kernel(
                     subtract(nc.gpsimd, next_s, fresh)
                     next_s += 1
             else:
-                ab_group(next_ab)
-                next_ab += 1
-                if next_s > j + S_AHEAD:
+                if next_ab < TILES:
+                    ab_group(next_ab)
+                    next_ab += 1
+                if j == BLOCK_ROUND:
+                    subtract(nc.gpsimd, next_s, "joined")
+                    next_s += 1
+                    idle.append(fresh)
+                elif j == rounds - 2:
+                    subtract(nc.gpsimd, next_s, fresh)
+                    next_s += 1
+                elif next_s > j + S_AHEAD + (j == rounds - 1):
                     idle.append(fresh)
                 elif j + 1 in runs and not quantises:
                     subtract(nc.gpsimd, next_s, idle.pop(0))
@@ -378,16 +420,17 @@ def tile_lazy_pruning_update_k3_kernel(
                 else:
                     subtract(nc.gpsimd, next_s, fresh)
                     next_s += 1
+            if j == BLOCK_ROUND - 1:
+                join_blocks()
             if j in copy_jobs:
                 interleave(nc.scalar.copy, *copy_jobs[j])
-        subtract(nc.gpsimd, next_s, idle.pop(0))
 
 
         last, n = TILES - 1, RANGES - 1
         for j in range(rounds, last - 1):
             finish(j)
             round_y(j)
-        finish(last - 1)
+        form_y(last - 1, [(first_cols, c_group(last - 1, "ab", first_cols))])
         copies = turn(rounds - GROUP, GROUP, "xt")
         round_y(last - 1)
         empty(nc.vector.tensor_copy, copies[:1])
@@ -402,4 +445,4 @@ def tile_lazy_pruning_update_k3_kernel(
         store_codes(n, GROUP, MTILES - 1)
         quantize_y(last, 1)
         store_codes(n, MTILES - 1, MTILES)
-        store_scales(n, [nc.sync, nc.scalar])
+        store_scales(n, 0)

@@ -76,6 +76,7 @@ def tile_lazy_pruning_update_k3_kernel(
         ident = kept("ident", [P, P], F32)
         y_codes = [kept("y_codes%d" % n, [P, ROWS], U32) for n in range(RANGES)]
         y_plane = [kept("y_plane%d" % n, [P, ROWS], U8) for n in range(RANGES)]
+        first_bf = [kept("first_bf%d" % k, [P, 2, 2, P, 2], BF16) for k in range(GROUP // 2)]
         blocks = kept("blocks", [P, GROUP, NT // 2], F32)
         block_codes = kept("block_codes", [P, 4, GROUP * QUAD], U32)
         block_plane = kept("block_plane", [P, GROUP * QUAD], U8)
@@ -198,17 +199,23 @@ def tile_lazy_pruning_update_k3_kernel(
             codes = b_codes[n][:, g, :] if n else b_head[g][:]
             mm(ab_acc[i][:], m, g, codes.bitcast(FP8X4), plane_of(b_first, n, g, B_ROW), g == 0, False)
 
-        def a_passes_and_t(i):
+        def a_passes(i):
             n, m = divmod(i, MTILES)
             for g in range(PASSES):
                 mm(ab_acc[i][:], m, g, a_codes[n][:, g, :].bitcast(FP4X4), plane_of(a_first, n, g, 0), False, g == PASSES - 1)
-            t_of[i] = work.tile([P, NT], F32, name="t", tag="t", bufs=T_BUFS)
-            nc.vector.tensor_tensor(out=t_of[i][:], in0=d_row[:, n, :], in1=ab_acc[i][:], op=MULT)
 
-        def ab_group(i):
+        def form_t(i):
+            t_of[i] = work.tile([P, NT], F32, name="t", tag="t", bufs=T_BUFS)
+            nc.vector.tensor_tensor(out=t_of[i][:], in0=d_row[:, i // MTILES, :], in1=ab_acc[i][:], op=MULT)
+
+        def ab_passes(i):
             for g in range(PASSES):
                 b_pass(i, g)
-            a_passes_and_t(i)
+            a_passes(i)
+
+        def ab_group(i):
+            ab_passes(i)
+            form_t(i)
 
         def subtract(engine, j, tag):
             n, m = divmod(j, MTILES)
@@ -239,6 +246,8 @@ def tile_lazy_pruning_update_k3_kernel(
             return ap.rearrange("r (p u e) -> r u p e", u=2, e=2)
 
         def new_rounded(j):
+            if j < GROUP:
+                return first_bf[j // 2][:, j % 2]
             y_bf[j] = work.tile([P, 2, P, 2], BF16, name="y_bf", tag="y_bf", bufs=BF_BUFS, align_bytes=64)
             return y_bf[j][:]
 
@@ -287,8 +296,9 @@ def tile_lazy_pruning_update_k3_kernel(
                 ))
             return copies
 
-        def turn_blocks(j):
-            nc.vector.transpose(out=blocks[:, j, :], in_=y_bf[j][:].rearrange("r u p e -> r (u p e)").bitcast(F32))
+        def turn_blocks(k):
+            words = first_bf[k][:].rearrange("r m u p e -> r (m u p e)").bitcast(F32)
+            nc.vector.transpose(out=blocks[:, 2 * k : 2 * k + 2, :].rearrange("p m x -> p (m x)"), in_=words)
 
         def join_blocks():
             y_grp[0] = work.tile([P, 4, GROUP * QUAD, 4], BF16, name="joined", tag="joined", bufs=1, align_bytes=64)
@@ -298,20 +308,20 @@ def tile_lazy_pruning_update_k3_kernel(
                 in_=blocks[:].rearrange("p m (u b r) -> p b m r u", u=2, b=4),
             )
 
-        def quantize_blocks():
-            for b in range(4):
-                nc.vector.quantize_mx(
-                    out=block_codes[:, b, :].bitcast(FP8X4), scales=block_plane[4 * b : P, :],
-                    in_=y_grp[0][:, b, :, :].rearrange("p x t -> p (x t)"),
-                )
-
-        def store_blocks(q):
+        def quantize_blocks(b):
+            nc.vector.quantize_mx(
+                out=block_codes[:, b, :].bitcast(FP8X4), scales=block_plane[4 * b : P, :],
+                in_=y_grp[0][:, b, :, :].rearrange("p x t -> p (x t)"),
+            )
             codes = out_1[0, :, : GROUP * P, :].rearrange("p (m q r) t -> q p m (r t)", q=4, r=QUAD)
-            scales = out_2[0, :, : GROUP * P].rearrange("i (m q r) -> q i m r", q=4, r=QUAD)
-            for b in range(4):
+            for q in range(4):
                 src = block_codes[QUAD * q : QUAD * (q + 1), b, :].rearrange("p (m r) -> p m r", r=QUAD)
                 move(nc.sync, codes[q, QUAD * b : QUAD * (b + 1)], src)
-            move(nc.sync, scales[q], block_plane[QUAD * q : QUAD * q + 16, :].rearrange("i (m r) -> i m r", r=QUAD))
+
+        def store_block_scales():
+            scales = out_2[0, :, : GROUP * P].rearrange("i (m q r) -> q i m r", q=4, r=QUAD)
+            for q in range(4):
+                move(nc.sync, scales[q], block_plane[QUAD * q : QUAD * q + 16, :].rearrange("i (m r) -> i m r", r=QUAD))
 
         def empty(engine_copy, copies):
             for dst, src in copies:
@@ -343,15 +353,17 @@ def tile_lazy_pruning_update_k3_kernel(
         for g in range(PASSES):
             interleave(nc.scalar.copy, 0, g, 1)
         for i in range(HEAD_TILES):
-            a_passes_and_t(i)
+            a_passes(i)
+            form_t(i)
         interleave(nc.vector.tensor_copy, 0, 0, 0)
         ab_group(HEAD_TILES)
         quantize_c(0, 0)
         ab_group(HEAD_TILES + 1)
         interleave(nc.vector.tensor_copy, 0, 1, 0)
-        ab_group(HEAD_TILES + 2)
+        ab_passes(HEAD_TILES + 2)
         quantize_c(0, 1)
         subtract(nc.vector, 0, "s_first")
+        form_t(HEAD_TILES + 2)
         for i in range(2 * HEAD_TILES, LEAD):
             ab_group(i)
         subtract(nc.gpsimd, 1, "handed_on")
@@ -367,13 +379,15 @@ def tile_lazy_pruning_update_k3_kernel(
         copy_jobs = {j: (1, g, h) for j, (g, h) in enumerate(halves)}
         copy_jobs.update({j: (2, g, h) for j, (g, h) in zip(late, halves)})
 
-        block_turns = dict(zip([j for j in range(1, MTILES) if j not in c_jobs], range(GROUP)))
+        block_turns = {2 * k + 3: k for k in range(GROUP // 2)}
+        free = [j for j in range(BLOCK_ROUND, rounds) if j not in c_jobs and j not in y_jobs]
+        block_jobs = dict(zip(free, range(4)))
         idle = ["s_spare"]
         next_ab, next_s = LEAD, S_AHEAD
         for j in range(rounds):
             finish(j)
             fresh = s_tag[j]
-            quantises = j in c_jobs or j in y_jobs
+            quantises = j in c_jobs or j in y_jobs or j in block_jobs
             if j not in runs:
                 round_y(j)
             if j in c_jobs:
@@ -386,16 +400,18 @@ def tile_lazy_pruning_update_k3_kernel(
                     store_scales(n, 0 if n else GROUP)
             if j in block_turns:
                 turn_blocks(block_turns[j])
-            if j == BLOCK_ROUND:
-                quantize_blocks()
-            if 0 <= j - BLOCK_ROUND < 4:
-                store_blocks(j - BLOCK_ROUND)
+            if j in block_jobs and j not in runs:
+                quantize_blocks(block_jobs[j])
+                if block_jobs[j] == 3:
+                    store_block_scales()
             if j in runs:
                 subtract(nc.vector, next_s, idle.pop(0))
                 next_s += 1
+                if j in block_jobs:
+                    quantize_blocks(block_jobs[j])
                 empty(nc.scalar.copy, turn(runs[j], GROUP, "xt"))
                 round_y(j)
-                if j + 1 in c_jobs:
+                if j + 1 in c_jobs or j + 1 in block_jobs:
                     idle.append(fresh)
                 else:
                     subtract(nc.gpsimd, next_s, fresh)
@@ -404,14 +420,7 @@ def tile_lazy_pruning_update_k3_kernel(
                 if next_ab < TILES:
                     ab_group(next_ab)
                     next_ab += 1
-                if j == BLOCK_ROUND:
-                    subtract(nc.gpsimd, next_s, "joined")
-                    next_s += 1
-                    idle.append(fresh)
-                elif j == rounds - 2:
-                    subtract(nc.gpsimd, next_s, fresh)
-                    next_s += 1
-                elif next_s > j + S_AHEAD + (j == rounds - 1):
+                if next_s > j + S_AHEAD and j < rounds - 2:
                     idle.append(fresh)
                 elif j + 1 in runs and not quantises:
                     subtract(nc.gpsimd, next_s, idle.pop(0))
@@ -420,7 +429,7 @@ def tile_lazy_pruning_update_k3_kernel(
                 else:
                     subtract(nc.gpsimd, next_s, fresh)
                     next_s += 1
-            if j == BLOCK_ROUND - 1:
+            if j == BLOCK_ROUND - 2:
                 join_blocks()
             if j in copy_jobs:
                 interleave(nc.scalar.copy, *copy_jobs[j])

from contextlib import ExitStack

import concourse.mybir as mybir

ROWS, BLK, REST = 1024, 1024, 1536
FLOPS = 3 * 2 * ROWS * BLK * REST

F32 = mybir.dt.float32
BF16 = mybir.dt.bfloat16
I32 = mybir.dt.int32
U32 = mybir.dt.uint32
U8 = mybir.dt.uint8
FP8X4 = mybir.dt.float8_e4m3fn_x4
FP4X4 = mybir.dt.float4_e2m1fn_x4
MULT = mybir.AluOpType.mult
ADD = mybir.AluOpType.add
SUB = mybir.AluOpType.subtract
EQUAL = mybir.AluOpType.is_equal

P = 128
NT = 512
QUAD = 32
PASSES = BLK // 512
MTILES = ROWS // P
RANGES = REST // NT
TILES = MTILES * RANGES
WIDE = REST - NT
D_WORDS = REST // P // 2
F_CHUNKS = [(0, 3), (3, 6), (6, 8)]
HEAD_TILES = F_CHUNKS[0][1]
V_ROWS = 2
B_ROW = 4
LEAD = MTILES
GROUP = 4
FIRST_RUN = GROUP + 1
LAST_ROUNDS = 4
S_AHEAD = 3
BLOCK_ROUND = MTILES - 1
WARM = 4
T_BUFS = LEAD + 1
Y_BUFS = 16
BF_BUFS = 2 * GROUP
GRP_BUFS = 5
C_BUFS = 3


def tile_lazy_pruning_update_k3_kernel(
    tc, f_words, f_scales, a_words, a_scales, b_words, b_scales, c, d, v, out_0, out_1, out_2
):
    nc = tc.nc
    with ExitStack() as ctx:
        keep = ctx.enter_context(tc.tile_pool(name="keep", bufs=1))
        work = ctx.enter_context(tc.tile_pool(name="work", bufs=1))
        psum = ctx.enter_context(tc.psum_pool(name="psum", bufs=1))
        ctx.enter_context(tc.manual_schedule())

        def kept(name, shape, dtype):
            return keep.tile(shape, dtype, name=name, align_bytes=64)

        f_plane = kept("f_plane", [P, PASSES, ROWS], U8)
        a_first = kept("a_first", [P, PASSES, NT], U8)
        b_first = kept("b_first", [P, PASSES, NT], U8)
        ab_rest = kept("ab_rest", [P, PASSES, WIDE], U8)
        f_head = [kept("f_head%d" % g, [P, HEAD_TILES * P], U32) for g in range(PASSES)]
        f_codes = {lo: kept("f_codes%d" % lo, [P, PASSES, (hi - lo) * P], U32) for lo, hi in F_CHUNKS[1:]}
        a_codes = [kept("a_codes%d" % n, [P, PASSES, 2 * NT], U8) for n in range(RANGES)]
        b_head = [kept("b_head%d" % g, [P, NT], U32) for g in range(PASSES)]
        b_codes = {n: kept("b_codes%d" % n, [P, PASSES, NT], U32) for n in range(1, RANGES)}
        c_raw = [[kept("c_raw%d_%d" % (n, g), [P, 4, NT], BF16) for g in range(PASSES)] for n in range(RANGES)]
        c_codes = [[kept("c_codes%d_%d" % (n, g), [P, NT], U32) for g in range(PASSES)] for n in range(RANGES)]
        c_plane = [[kept("c_plane%d_%d" % (n, g), [P, NT], U8) for g in range(PASSES)] for n in range(RANGES)]
        v_first = [kept("v_first%d" % h, [P, V_ROWS, NT], BF16) for h in range(MTILES // V_ROWS)]
        v_wide = [kept("v_wide%d" % h, [P, V_ROWS, WIDE], BF16) for h in range(MTILES // V_ROWS)]
        d_col = kept("d_col", [P, REST // P], BF16)
        d_row = kept("d_row", [P, RANGES, NT], BF16)
        ident = kept("ident", [P, P], F32)
        y_codes = [kept("y_codes%d" % n, [P, ROWS], U32) for n in range(RANGES)]
        y_plane = [kept("y_plane%d" % n, [P, ROWS], U8) for n in range(RANGES)]
        first_bf = [kept("first_bf%d" % k, [P, 2, 2, P, 2], BF16) for k in range(GROUP // 2)]
        blocks = kept("blocks", [P, GROUP, NT // 2], F32)
        block_codes = kept("block_codes", [P, 4, GROUP * QUAD], U32)
        block_plane = kept("block_plane", [P, GROUP * QUAD], U8)

        f_view = f_words.rearrange("g p m t -> p g (m t)")
        a_view = a_words.rearrange("g p x -> p g x")
        b_view = b_words.rearrange("g p n t -> p g (n t)")
        first_cols, wide_cols = slice(0, NT), slice(NT, REST)


        def move(queue, dst, src):
            queue.dma_start(out=dst.bitcast(I32), in_=src.bitcast(I32))

        def load_scales(queue, plane, scales, first_row):
            for q in range(4):
                lo = QUAD * q + first_row
                move(queue, plane[lo : lo + 4, :, :], scales[:, 4 * q : 4 * q + 4, :].rearrange("g r n -> r g n"))

        def load_f(chunk):
            lo, hi = F_CHUNKS[chunk]
            move(nc.sync, f_codes[lo][:], f_view[:, :, 4 * P * lo : 4 * P * hi])

        def load_a(queue, n):
            move(queue, a_codes[n][:], a_view[:, :, 2 * NT * n : 2 * NT * (n + 1)])

        def load_b(n):
            move(nc.sync, b_codes[n][:], b_view[:, :, 4 * NT * n : 4 * NT * (n + 1)])

        def load_c(n, g):
            rows = c[512 * g : 512 * (g + 1), NT * n : NT * (n + 1)]
            nc.sync.dma_start(out=c_raw[n][g][:], in_=rows.rearrange("(p j) w -> p j w", j=4))

        def load_v(tiles, h, cols):
            rows = v[P * V_ROWS * h : P * V_ROWS * (h + 1), cols]
            nc.sync.dma_start(out=tiles[h][:], in_=rows.rearrange("(m p) w -> p m w", p=P))

        def zero(plane):
            nc.vector.memset(plane[:].rearrange("p g n -> p (g n)").bitcast(I32), 0)

        def build_identity():
            ones = kept("ones", [P, QUAD], F32)
            ramp = kept("ramp", [P, QUAD], F32)
            ramp_turned = kept("ramp_turned", [P, QUAD], F32)
            nc.vector.memset(ones[:], 1.0)
            nc.vector.memset(ident[:], 0.0)
            nc.vector.tensor_tensor_scan(out=ramp[:], data0=ones[:], data1=ones[:], initial=0.0, op0=MULT, op1=ADD)
            nc.vector.transpose(out=ramp_turned[:], in_=ramp[:])
            for q in range(P // QUAD):
                rows = slice(QUAD * q, QUAD * (q + 1))
                nc.vector.tensor_tensor(out=ident[rows, rows], in0=ramp[rows, :], in1=ramp_turned[rows, :], op=EQUAL)

        move(nc.gpsimd, b_head[0][:], b_view[:, 0, : 4 * NT])
        load_a(nc.gpsimd, 0)
        zero(f_plane)
        zero(b_first)
        build_identity()
        zero(a_first)
        zero(ab_rest)
        load_scales(nc.gpsimd, ab_rest, b_scales[:, :, wide_cols], B_ROW)

        nc.sync.dma_start(out=d_col[:], in_=d.rearrange("(p j) -> p j", p=P))
        move(nc.sync, f_head[0][:], f_view[:, 0, : 4 * P * HEAD_TILES])
        load_scales(nc.sync, f_plane, f_scales, 0)
        load_scales(nc.sync, b_first, b_scales[:, :, first_cols], B_ROW)
        move(nc.sync, f_head[1][:], f_view[:, 1, : 4 * P * HEAD_TILES])
        move(nc.sync, b_head[1][:], b_view[:, 1, : 4 * NT])
        load_scales(nc.sync, a_first, a_scales[:, :, first_cols], 0)
        for g in range(PASSES):
            load_f(1 + g)
            load_c(0, g)
        load_scales(nc.sync, ab_rest, a_scales[:, :, wide_cols], 0)
        load_v(v_first, 0, first_cols)
        load_b(1)
        load_a(nc.sync, 1)
        load_v(v_first, 1, first_cols)
        load_c(1, 0)
        load_v(v_first, 2, first_cols)
        load_v(v_first, 3, first_cols)
        load_c(1, 1)
        load_v(v_wide, 0, wide_cols)
        load_v(v_wide, 1, wide_cols)
        load_b(2)
        load_a(nc.sync, 2)
        for g in range(PASSES):
            load_c(2, g)
            load_v(v_wide, 2 + g, wide_cols)


        def bank(kind):
            return psum.tile([P, NT], F32, name=kind, tag=kind, bufs={"ab": 3, "c": 3, "xt": 2}[kind])

        def spread_d():
            d_words = d_col[:].bitcast(F32)
            d_row_words = d_row[:].rearrange("r n w -> r (n w)").bitcast(F32).rearrange("r (p w) -> r p w", p=P)
            for lo, hi in ((0, NT // P), (NT // P, D_WORDS)):
                xt = bank("xt")
                for w in range(lo, hi):
                    slot = slice(P * (w - lo), P * (w - lo + 1))
                    nc.tensor.transpose(xt[:, slot], d_words[:, w : w + 1].to_broadcast([P, P]), ident[:])
                nc.scalar.copy(out=d_row_words[:, :, lo:hi], in_=xt[:, : P * (hi - lo)].rearrange("r (w p) -> r p w", p=P))

        def mm(acc, m, g, rhs, rhs_scale, start, stop):
            lo = max(first for first, end in F_CHUNKS if first <= m)
            cols = slice(P * (m - lo), P * (m - lo + 1))
            codes = f_codes[lo][:, g, cols] if lo else f_head[g][:, cols]
            nc.tensor.matmul_mx(
                out=acc, lhsT=codes.bitcast(FP8X4), lhsT_scale=f_plane[:, g, P * m : P * (m + 1)],
                rhs=rhs, rhs_scale=rhs_scale, start=start, stop=stop,
            )

        ab_acc, t_of, s_of, s_tag, y_of, y_bf, y_grp, c_grp = {}, {}, {}, {}, {}, {}, {}, {}

        def plane_of(first, n, g, row):
            return first[row:P, g, :] if n == 0 else ab_rest[row:P, g, NT * (n - 1) : NT * n]

        def b_pass(i, g):
            n, m = divmod(i, MTILES)
            if g == 0:
                ab_acc[i] = bank("c" if HEAD_TILES <= i < 2 * HEAD_TILES else "ab")
            codes = b_codes[n][:, g, :] if n else b_head[g][:]
            mm(ab_acc[i][:], m, g, codes.bitcast(FP8X4), plane_of(b_first, n, g, B_ROW), g == 0, False)

        def a_passes(i):
            n, m = divmod(i, MTILES)
            for g in range(PASSES):
                mm(ab_acc[i][:], m, g, a_codes[n][:, g, :].bitcast(FP4X4), plane_of(a_first, n, g, 0), False, g == PASSES - 1)

        def form_t(i):
            t_of[i] = work.tile([P, NT], F32, name="t", tag="t", bufs=T_BUFS)
            nc.vector.tensor_tensor(out=t_of[i][:], in0=d_row[:, i // MTILES, :], in1=ab_acc[i][:], op=MULT)

        def ab_passes(i):
            for g in range(PASSES):
                b_pass(i, g)
            a_passes(i)

        def ab_group(i):
            ab_passes(i)
            form_t(i)

        def subtract(engine, j, tag):
            n, m = divmod(j, MTILES)
            h, row = divmod(m, V_ROWS)
            v_tile = v_wide[h][:, row, NT * (n - 1) : NT * n] if n else v_first[h][:, row, :]
            s_tag[j] = tag
            s_of[j] = work.tile([P, NT], F32, name=tag, tag=tag, bufs=1, align_bytes=64)
            engine.tensor_tensor(out=s_of[j][:], in0=v_tile, in1=t_of[j][:], op=SUB)

        def c_group(j, kind, cols):
            n, m = divmod(j, MTILES)
            acc = bank(kind)[:, : cols.stop - cols.start]
            for g in range(PASSES):
                mm(acc, m, g, c_codes[n][g][:, cols].bitcast(FP8X4), c_plane[n][g][:, cols], g == 0, g == PASSES - 1)
            return acc

        def form_y(j, parts):
            n, m = divmod(j, MTILES)
            y_of[j] = work.tile([P, NT], F32, name="y", tag="y", bufs=Y_BUFS)
            for cols, acc in parts:
                nc.vector.tensor_tensor(out=y_of[j][:, cols], in0=s_of[j][:, cols], in1=acc, op=SUB)
            nc.sync.dma_start(out=out_0[P * m : P * (m + 1), NT * n : NT * (n + 1)], in_=y_of[j][:])

        def finish(j):
            form_y(j, [(first_cols, c_group(j, "c", first_cols))])

        def word_order(ap):
            return ap.rearrange("r (p u e) -> r u p e", u=2, e=2)

        def new_rounded(j):
            if j < GROUP:
                return first_bf[j // 2][:, j % 2]
            y_bf[j] = work.tile([P, 2, P, 2], BF16, name="y_bf", tag="y_bf", bufs=BF_BUFS, align_bytes=64)
            return y_bf[j][:]

        def round_y(j):
            nc.scalar.copy(out=new_rounded(j), in_=word_order(y_of[j][:]))

        def finish_last(j):
            halves = [slice(0, NT // 2), slice(NT // 2, NT)]
            parts = [(cols, c_group(j, "ab", cols)) for cols in halves]
            rounded = new_rounded(j)
            for h, (cols, acc) in enumerate(parts):
                words = rounded[:, :, h * P // 2 : (h + 1) * P // 2, :]
                nc.vector.tensor_tensor(out=words, in0=word_order(s_of[j][:, cols]), in1=word_order(acc), op=SUB)
            form_y(j, parts)

        def interleave(engine_copy, n, g, h):
            if (n, g) not in c_grp:
                tag, bufs = ("handed_on", 1) if (n, g) == (0, PASSES - 1) else ("c_grp", C_BUFS)
                c_grp[n, g] = work.tile([P, NT, 4], BF16, name="c_grp", tag=tag, bufs=bufs, align_bytes=64)
            cols = slice(h * NT // 2, (h + 1) * NT // 2)
            engine_copy(
                out=c_grp[n, g][:, cols, :].rearrange("p (c i) t -> p c t i", i=4),
                in_=c_raw[n][g][:, :, cols].rearrange("p t (c i) -> p c t i", i=4),
            )

        def quantize_c(n, g):
            nc.vector.quantize_mx(
                out=c_codes[n][g][:].bitcast(FP8X4), scales=c_plane[n][g][:], in_=c_grp[n, g][:].rearrange("p w t -> p (w t)")
            )

        def turn(first, count, kind):
            y_grp[first] = work.tile([P, count * P, 4], BF16, name="y_grp", tag="y_grp", bufs=GRP_BUFS, align_bytes=64)
            grp_words = y_grp[first][:].rearrange("p m t -> p (m t)").bitcast(F32)
            copies = []
            for lo in range(0, count, 2):
                xt = bank(kind)
                span = min(2, count - lo)
                for s in range(span):
                    words = y_bf[first + lo + s][:].rearrange("r u p e -> r (u p e)").bitcast(F32)
                    for u in range(2):
                        slot = 2 * s + u
                        nc.tensor.transpose(xt[:, P * slot : P * (slot + 1)], words[:, P * u : P * (u + 1)], ident[:])
                copies.append((
                    grp_words[:, 2 * P * lo : 2 * P * (lo + span)].rearrange("p (s r u) -> p s r u", r=P, u=2),
                    xt[:, : 2 * P * span].rearrange("p (s u r) -> p s r u", r=P, u=2),
                ))
            return copies

        def turn_blocks(k):
            words = first_bf[k][:].rearrange("r m u p e -> r (m u p e)").bitcast(F32)
            nc.vector.transpose(out=blocks[:, 2 * k : 2 * k + 2, :].rearrange("p m x -> p (m x)"), in_=words)

        def join_blocks():
            y_grp[0] = work.tile([P, 4, GROUP * QUAD, 4], BF16, name="joined", tag="joined", bufs=1, align_bytes=64)
            words = y_grp[0][:].rearrange("p b x t -> p (b x t)").bitcast(F32)
            nc.scalar.copy(
                out=words.rearrange("p (b m r u) -> p b m r u", b=4, m=GROUP, u=2),
                in_=blocks[:].rearrange("p m (u b r) -> p b m r u", u=2, b=4),
            )

        def quantize_blocks(b):
            nc.vector.quantize_mx(
                out=block_codes[:, b, :].bitcast(FP8X4), scales=block_plane[4 * b : P, :],
                in_=y_grp[0][:, b, :, :].rearrange("p x t -> p (x t)"),
            )
            codes = out_1[0, :, : GROUP * P, :].rearrange("p (m q r) t -> q p m (r t)", q=4, r=QUAD)
            for q in range(4):
                src = block_codes[QUAD * q : QUAD * (q + 1), b, :].rearrange("p (m r) -> p m r", r=QUAD)
                move(nc.sync, codes[q, QUAD * b : QUAD * (b + 1)], src)

        def store_block_scales():
            scales = out_2[0, :, : GROUP * P].rearrange("i (m q r) -> q i m r", q=4, r=QUAD)
            for q in range(4):
                move(nc.sync, scales[q], block_plane[QUAD * q : QUAD * q + 16, :].rearrange("i (m r) -> i m r", r=QUAD))

        def empty(engine_copy, copies):
            for dst, src in copies:
                engine_copy(out=dst, in_=src)

        def quantize_y(first, count):
            n, m = divmod(first, MTILES)
            cols = slice(P * m, P * (m + count))
            nc.vector.quantize_mx(
                out=y_codes[n][:, cols].bitcast(FP8X4), scales=y_plane[n][:, cols],
                in_=y_grp[first][:].rearrange("p m t -> p (m t)"),
            )

        def store_codes(n, lo, hi):
            move(nc.sync, out_1[n].rearrange("p m t -> p (m t)")[:, 4 * P * lo : 4 * P * hi], y_codes[n][:, P * lo : P * hi])

        def store_scales(n, lo):
            for q in range(4):
                move(nc.sync, out_2[n, 4 * q : 4 * q + 4, P * lo :], y_plane[n][QUAD * q : QUAD * q + 4, P * lo :])


        spread_d()
        warm = bank("c")
        for k in range(WARM):
            mm(warm[:, : 2 * P], 0, 0, f_head[0][:, : 2 * P].bitcast(FP8X4), f_plane[:, 0, : 2 * P], True, True)
        for g in range(PASSES):
            for i in range(HEAD_TILES):
                b_pass(i, g)
        for g in range(PASSES):
            interleave(nc.scalar.copy, 0, g, 1)
        for i in range(HEAD_TILES):
            a_passes(i)
            form_t(i)
        interleave(nc.vector.tensor_copy, 0, 0, 0)
        ab_group(HEAD_TILES)
        quantize_c(0, 0)
        ab_group(HEAD_TILES + 1)
        interleave(nc.vector.tensor_copy, 0, 1, 0)
        ab_passes(HEAD_TILES + 2)
        quantize_c(0, 1)
        subtract(nc.vector, 0, "s_first")
        form_t(HEAD_TILES + 2)
        for i in range(2 * HEAD_TILES, LEAD):
            ab_group(i)
        subtract(nc.gpsimd, 1, "handed_on")
        subtract(nc.gpsimd, 2, "s_third")


        rounds = TILES - LAST_ROUNDS
        runs = {FIRST_RUN + first: first for first in range(GROUP, rounds - FIRST_RUN, GROUP)}
        y_jobs = {j + (1 if j == max(runs) else 2): first for j, first in runs.items()}
        c_jobs = {MTILES * n - 4 + 2 * g: (n, g) for n in range(1, RANGES) for g in range(PASSES)}
        halves = [(g, h) for g in range(PASSES) for h in range(2)]
        late = [j for j in range(MTILES - 1, rounds) if j not in runs]
        copy_jobs = {j: (1, g, h) for j, (g, h) in enumerate(halves)}
        copy_jobs.update({j: (2, g, h) for j, (g, h) in zip(late, halves)})

        block_turns = {2 * k + 3: k for k in range(GROUP // 2)}
        free = [j for j in range(BLOCK_ROUND, rounds) if j not in c_jobs and j not in y_jobs]
        block_jobs = dict(zip(free, range(4)))
        idle = ["s_spare"]
        next_ab, next_s = LEAD, S_AHEAD
        for j in range(rounds):
            finish(j)
            fresh = s_tag[j]
            quantises = j in c_jobs or j in y_jobs or j in block_jobs
            if j not in runs:
                round_y(j)
            if j in c_jobs:
                quantize_c(*c_jobs[j])
            if j in y_jobs:
                n, m = divmod(y_jobs[j], MTILES)
                quantize_y(y_jobs[j], GROUP)
                store_codes(n, m, m + GROUP)
                if m:
                    store_scales(n, 0 if n else GROUP)
            if j in block_turns:
                turn_blocks(block_turns[j])
            if j in block_jobs and j not in runs:
                quantize_blocks(block_jobs[j])
                if block_jobs[j] == 3:
                    store_block_scales()
            if j in runs:
                subtract(nc.vector, next_s, idle.pop(0))
                next_s += 1
                if j in block_jobs:
                    quantize_blocks(block_jobs[j])
                empty(nc.scalar.copy, turn(runs[j], GROUP, "xt"))
                round_y(j)
                if j + 1 in c_jobs or j + 1 in block_jobs:
                    idle.append(fresh)
                else:
                    subtract(nc.gpsimd, next_s, fresh)
                    next_s += 1
            else:
                if next_ab < TILES:
                    ab_group(next_ab)
                    next_ab += 1
                if next_s > j + S_AHEAD and j < rounds - 2:
                    idle.append(fresh)
                elif j + 1 in runs and not quantises:
                    subtract(nc.gpsimd, next_s, idle.pop(0))
                    idle.append(fresh)
                    next_s += 1
                else:
                    subtract(nc.gpsimd, next_s, fresh)
                    next_s += 1
            if j == BLOCK_ROUND - 2:
                join_blocks()
            if j in copy_jobs:
                interleave(nc.scalar.copy, *copy_jobs[j])


        last, n = TILES - 1, RANGES - 1
        for j in range(rounds, last - 1):
            finish(j)
            round_y(j)
        form_y(last - 1, [(first_cols, c_group(last - 1, "ab", first_cols))])
        copies = turn(rounds - GROUP, GROUP, "xt")
        round_y(last - 1)
        empty(nc.vector.tensor_copy, copies[:1])
        empty(nc.scalar.copy, copies[1:])
        finish_last(last)
        for first, count in ((rounds, 2), (last - 1, 1), (last, 1)):
            empty(nc.scalar.copy, turn(first, count, "c"))
        quantize_y(rounds - GROUP, GROUP)
        store_codes(n, 0, GROUP)
        quantize_y(rounds, 2)
        quantize_y(last - 1, 1)
        store_codes(n, GROUP, MTILES - 1)
        quantize_y(last, 1)
        store_codes(n, MTILES - 1, MTILES)
        store_scales(n, 0)
